import numpy as np, ml_dtypes
CORES = [13,21,141,149]
N = 4
BF = ml_dtypes.bfloat16
def gentries(a):
    return np.ascontiguousarray(a.reshape(8, 16, -1).transpose(0, 2, 1)).reshape(8, -1)
def gtable(e):
    e = np.asarray(e); return np.ascontiguousarray(e.reshape(8, -1, 16).transpose(0, 2, 1)).reshape(128, -1).astype(np.int32)
L, XW, YW, R, SL = 2, 64, 32, 1024, 48
C = XW * YW
SLR = np.arange(128) % 16 >= 14
def pack(e, fc, x, v, u, w):
    g = lambda a: np.stack([gtable(t) for t in a])
    return {"lay": e.astype(np.float32).astype(BF), "fac": np.repeat(fc, 16, axis=1).astype(np.int32), "px": g(x), "py": g(v), "dx": g(u), "dy": g(w)}
def parts(rng):
    e = rng.integers(-120, 121, (N, 128, L * C), dtype=np.int16)
    e[:, SLR] = rng.integers(-SL, SL + 1, (N, 16, L * C), dtype=np.int16)
    fc = np.stack([np.stack([rng.permutation(16)[:8] + 1 for l in range(L)], axis=1) for r in range(N)])
    return [e, fc, rng.integers(0, 16 * XW, (N, 8, R)), rng.integers(0, 16 * YW, (N, 8, R)), rng.integers(-16, 17, (N, 8, R)), rng.integers(-16, 17, (N, 8, R))]
def setup_inputs(rng):
    return pack(*parts(rng))
def setup_inputs_prism(rng):
    e, fc, x, v, u, w = parts(rng)
    return pack(np.tile(e[:, :16], (1, 8, 1)), fc, *[np.repeat(a[:, :1], 8, axis=1) for a in (x, v, u, w)])
def setup_inputs_steep(rng):
    e, fc, x, v, u, w = parts(rng); g = int(rng.integers(0, 8))
    e[:, SLR] = SL * rng.choice(np.array([-1, 1]), (N, 16, L * C)); fc[:] = 16
    u = 16 * rng.choice(np.array([-1, 1]), u.shape); w = 16 * rng.choice(np.array([-1, 1]), w.shape)
    e[:, 16 * g] = 120; e[:, 16 * g + 1] = -120; e[:, 16 * g + 14] = SL; e[:, 16 * g + 15] = -SL; u[:, g] = 16; w[:, g] = -16
    return pack(e, fc, x, v, u, w)
def setup_inputs_edges(rng):
    e, fc, x, v, u, w = parts(rng)
    e[:, SLR] = rng.choice(np.array([-8, -1, 0, 1, 8]), (N, 16, L * C)); fc = rng.choice(np.array([1, 2, 15, 16]), fc.shape)
    x = rng.choice(np.array([0, 15, 16, 16 * XW - 16, 16 * XW - 1]), x.shape); v = rng.choice(np.array([0, 15, 16, 16 * YW - 16, 16 * YW - 1]), v.shape)
    u = rng.choice(np.array([-16, -1, 0, 1, 16]), u.shape); w = rng.choice(np.array([-16, -1, 0, 1, 16]), w.shape)
    return pack(e, fc, x, v, u, w)
def setup_inputs_one(rng):
    p = parts(rng); q = int(rng.integers(0, N))
    for i in range(2, 6):
        p[i] = np.repeat(p[i][:, :, :16], R // 16, axis=2); p[i][q] = p[i][q][:, :1]
    return pack(*p)
def setup_inputs_spread(rng):
    e, fc, x, v, u, w = parts(rng)
    z = rng.random(e.shape, dtype=np.float32); e[z < 0.5] = 0; k = z > 0.9; b = np.where(SLR, SL, 120)[None, :, None]
    e = np.where(k, np.where(e < 0, -b, b), e)
    x = np.floor(rng.random(x.shape) ** 4 * (16 * XW)).astype(np.int64); v = np.floor(rng.random(v.shape) ** 4 * (16 * YW)).astype(np.int64)
    return pack(e, fc, x, v, u, w)
def check_inputs(d):
    bad = []; e = d["lay"].astype(np.float32); fc = d["fac"]
    if not np.array_equal(e, np.floor(e)): bad.append("whole numbers in lay")
    if not np.abs(e[:, ~SLR]).max() <= 120: bad.append("emission")
    if not np.abs(e[:, SLR]).max() <= SL: bad.append("slopes")
    if not (fc.min() >= 1 and fc.max() <= 16): bad.append("factors")
    if not np.array_equal(fc, np.repeat(fc[:, ::16], 16, axis=1)): bad.append("factors alike in a group")
    if not (d["px"].min() >= 0 and d["px"].max() < 16 * XW and d["py"].min() >= 0 and d["py"].max() < 16 * YW): bad.append("places")
    if not (min(d["dx"].min(), d["dy"].min()) >= -16 and max(d["dx"].max(), d["dy"].max()) <= 16): bad.append("directions")
    return bad
def reference(lay, fac, px, py, dx, dy):
    t = lay.astype(np.float32).astype(np.int32).reshape(N, 8, 16, L, C)
    y = np.zeros((N, 128, R), np.float32); g8 = np.arange(8)[:, None, None]; c16 = np.arange(16)[None, :, None]
    for r in range(N):
        x, v, u, w = [gentries(a[r]).astype(np.int64) for a in (px, py, dx, dy)]
        s = np.zeros((8, 16, R), np.int64)
        for h in range(N):
            q = (r + h) % N
            for l in range(L):
                fc = fac[q, ::16, l].astype(np.int64)[:, None]
                cell = (v >> 4) * XW + (x >> 4)
                p = t[q][g8, c16, l, cell[:, None, :]].astype(np.int64)
                s = s + p
                u = u + ((fc * p[:, 14]) >> 7); w = w + ((fc * p[:, 15]) >> 7)
                x = (x + u) & (16 * XW - 1); v = (v + w) & (16 * YW - 1)
        y[r] = s.reshape(128, R).astype(np.float32)
    return {"y": y}

@@ -1,0 +1,343 @@
+from concourse.bass import DstId, RemoteDMATransfer
+from concourse.mybir import AluOpType, AxisListType, ActivationFunctionType
+
+R, NL = 1024, 64
+CELLS = 2048
+SEL = 32
+TAB = SEL + 2 * CELLS
+BIAS = 1024
+HALF = 127.0 / 256.0
+SPLIT = 32
+
+SCRATCH = {
+    "taba": ("sbuf", [128, TAB], "bfloat16"),
+    "tabb": ("sbuf", [128, TAB], "bfloat16"),
+    "gat": ("sbuf", [128, 8 * R], "bfloat16"),
+    "rays": ("sbuf", [128, 4 * NL], "int32"),
+    "faci": ("sbuf", [128, 4], "int32"),
+    "facf": ("sbuf", [128, 4], "float32"),
+    "iot": ("sbuf", [128, 272], "float32"),
+    "selb": ("sbuf", [128, 16], "float32"),
+    "e01": ("sbuf", [128, 128], "float32"),
+    "e2": ("sbuf", [128, 64], "float32"),
+    "mk": ("sbuf", [128, 4], "float32"),
+    "eh": ("sbuf", [128, 64], "float16"),
+    "rr": ("sbuf", [128, 256], "bfloat16"),
+    "idb": ("sbuf", [128, 128], "bfloat16"),
+    "idh": ("sbuf", [128, 128], "float16"),
+    "lt": ("sbuf", [128, 512], "float16"),
+    "idx": ("sbuf", [128, 8 * NL], "uint16"),
+    "pos": ("sbuf", [128, 10 * 128], "int32"),
+    "wf": ("sbuf", [128, 8 * 128], "float32"),
+    "tw": ("sbuf", [128, 128], "float32"),
+    "msk": ("sbuf", [128, 128], "int32"),
+    "cv": ("sbuf", [128, 33, 8], "bfloat16"),
+    "mo1": ("sbuf", [128, 256], "uint16"),
+    "mi1": ("sbuf", [128, 256], "uint16"),
+    "mo2": ("sbuf", [128, 192], "uint16"),
+    "mi2": ("sbuf", [128, 192], "uint16"),
+    "pout": ("sbuf", [128, R], "float16"),
+    "pin": ("sbuf", [128, R], "float16"),
+    "res": ("sbuf", [128, R], "float32"),
+    "sa0": ("psum", [128, 512], "float32"),
+    "sa1": ("psum", [128, 512], "float32"),
+    "sc0": ("psum", [128, 512], "float32"),
+    "sc1": ("psum", [128, 512], "float32"),
+    "ps1": ("psum", [128, 512], "float32"),
+    "ps2": ("psum", [128, 512], "float32"),
+    "psi": ("psum", [128, 512], "float32"),
+}
+SEMAPHORES = ["ld0", "ld1", "ld2", "ld3", "ldf", "ldp", "fz", "io0", "io1", "io2", "io3", "v", "selr", "cst", "ltr",
+              "pei", "idxr", "gs", "gv", "pe1", "cvt", "pe2", "m1r", "m2r", "pr0", "pr1", "c0", "c1", "a0", "a1",
+              "arr0", "arr1", "am1", "am2", "ap0", "ap1", "sent", "hp0", "hp1", "cp0", "cp1", "st0", "st1"]
+
+A = AluOpType
+
+
+def piece(i):
+    if i < 4:
+        w = (CELLS + SEL) // 4
+        return w * i, w * (i + 1)
+    return SEL + 512 * i, SEL + 512 * (i + 1)
+
+
+def helpers_of(src, dst, T, topo):
+    hs = [h for h in topo.cores_of(src) if T.rank_of(h) is None and topo.may_write(h, dst)]
+    far = [h for h in hs if topo.die(h) != topo.die(src)]
+    near = [h for h in hs if topo.die(h) == topo.die(src)]
+    out = []
+    for i in range(max(len(far), len(near))):
+        out += far[i:i + 1] + near[i:i + 1]
+    return out
+
+
+def helper_program(g, core, T, topo):
+    n = len(T.cores)
+    for q in range(n):
+        src, dst = T.cores[q], T.cores[(q + 1) % n]
+        hs = helpers_of(src, dst, T, topo)
+        if core not in hs:
+            continue
+        rid, pid = topo.addr(dst, core)
+        ne_in, ne_out = len(topo.engines(src, core)) // 2, len(topo.engines(core, dst))
+        got, sent = [0, 0], 0
+        for i in range(8):
+            if hs[i % len(hs)] != core:
+                continue
+            lay = i // 4
+            a, b = piece(i)
+            got[lay] += ne_in
+            g.wait_ge(T.sem["hp%d" % lay], got[lay])
+            g.remote_dma(T.tabb[:, a:b], T.taba[:, a:b], T.sem["arr%d" % lay], T.sem.sent, pid, rid, topo.mask(core, dst))
+            sent += ne_out
+        g.wait_ge(T.sem.sent, sent)
+
+
+def rank_program(g, core, T, topo):
+    rank = T.rank_of(core)
+    if rank is None:
+        helper_program(g, core, T, topo)
+        return
+    n = len(T.cores)
+    nxt, partner, prev = T.cores[(rank + 1) % n], T.cores[(rank + 2) % n], T.cores[(rank - 1) % n]
+    V, S, PE, SY = g.vector, g.scalar, g.tensor, g.sync
+    cnt = {}
+
+    def inc(ins, name, k=1):
+        ins.then_inc(T.sem[name], k)
+        cnt[name] = cnt.get(name, 0) + k
+
+    def wait(q, *names):
+        for name in names:
+            q.wait_ge(T.sem[name], cnt[name])
+
+    def ts(out, in0, s1, op0, s2=None, op1=None):
+        if op1 is None:
+            return V.tensor_scalar(out, in0, s1, None, op0)
+        return V.tensor_scalar(out, in0, s1, s2, op0, op1)
+
+    def load_tab(q, i):
+        a, b = piece(2 * i)[0], min(piece(2 * i + 1)[1], CELLS if i < 2 else TAB)
+        o = 0 if i < 2 else SEL
+        inc(q.dma_start(T.taba[:, a:b], T.lay[:, a - o:b - o]), "ld%d" % i, 16)
+    inc(V.memset(T.faci[:, :], 0), "fz")
+    load_tab(SY, 0)
+    inc(S.dma_start(T.rays[64:96, :], T.dx[:, :]), "ldp", 16)
+    inc(SY.dma_start(T.rays[0:32, :], T.px[:, :]), "ldp", 16)
+    inc(S.dma_start(T.rays[96:128, :], T.dy[:, :]), "ldp", 16)
+    inc(SY.dma_start(T.rays[32:64, :], T.py[:, :]), "ldp", 16)
+    wait(S, "fz")
+    for uv in range(2):
+        inc(S.dma_start(T.faci[14 + uv::16, 0:2], T.fac[14 + uv::16, :]), "ldf", 16)
+    load_tab(SY, 1)
+    load_tab(S, 2)
+    load_tab(SY, 3)
+
+    def iota(out, pattern, base, cm, name):
+        inc(g.iota(out, pattern, base, cm, allow_small_or_imprecise_dtypes=True), name)
+    iota(T.iot[:, 16:80], [[-1, 2], [-32, 4], [-4, 8]], 0, 1, "io1")
+    iota(T.iot[:, 0:16], [[1, 2], [16, 8]], 14, -1, "io0")
+    iota(T.iot[:, 80:144], [[-2, 64]], 0, 1, "io2")
+    iota(T.iot[:, 144:272], [[-1, 128]], 0, 1, "io3")
+    inc(V.memset(T.cv[:, :, :], 0.0), "v")
+    wait(V, "io1")
+    for h in range(2):
+        inc(ts(T.e01[:, 64 * h:64 * h + 64], T.iot[:, 16:80], 2.0 * h, A.is_equal), "v")
+    wait(V, "io0")
+    inc(ts(T.selb[:, :], T.iot[:, 0:16], 0.0, A.is_equal, 1.0 / 128.0, A.mult), "v")
+    wait(V, "v")
+    for h in range(2):
+        inc(V.tensor_reduce(T.mk[:, h:h + 1], T.e01[:, 64 * h:64 * h + 64], AxisListType.X, A.add), "v")
+    inc(V.tensor_tensor(T.e2[:, :], T.e01[:, 0:64], T.e01[:, 64:128], A.add), "v")
+    wait(V, "v")
+    for c2 in range(2):
+        o = 32 * c2
+        inc(V.tensor_copy(T.eh[:, o:o + 16], T.e2[:, o:o + 16]), "cst")
+        inc(V.tensor_tensor(T.eh[:, o + 16:o + 32], T.e2[:, o:o + 16], T.e2[:, o + 16:o + 32], A.add), "cst")
+    wait(V, "io2")
+    for uv in range(2):
+        for h in range(2):
+            c = 128 * uv + 64 * h
+            inc(ts(T.rr[:, c:c + 64], T.iot[:, 80:144], float(h), A.is_equal, 4.0 if uv else 1.0, A.mult), "cst")
+    wait(V, "ldp")
+    for h in range(2):
+        inc(ts(T.lt[:, h::2], T.rays[:, :], T.mk[:, h:h + 1], A.mult), "ltr")
+    wait(PE, "cst", "ltr")
+    for ch in range(8):
+        c2, c4 = ch // 4, ch % 4
+        inc(PE.matmul(T.psi[:, ch:256:8], T.lt[:, 128 * c4:128 * c4 + 128], T.eh[:, 32 * c2:32 * c2 + 32], True, True), "pei")
+    wait(V, "ldf")
+    inc(V.tensor_copy(T.facf[:, 0:2], T.faci[:, 0:2]), "v")
+    wait(V, "io3")
+    inc(ts(T.idb[:, :], T.iot[:, 144:272], 0.0, A.is_equal), "cst")
+    wait(V, "v")
+    for l in range(2):
+        inc(ts(T.taba[:, CELLS + 16 * l:CELLS + 16 * l + 16], T.selb[:, :], T.facf[:, l:l + 1], A.mult), "selr")
+
+    hs = helpers_of(core, nxt, T, topo)
+    cnt["sent"] = 0
+    for i in range(4):
+        wait(g, "ld%d" % i)
+        if i == 1:
+            wait(g, "selr")
+        trs = []
+        for j in range(2):
+            h = hs[(2 * i + j) % len(hs)]
+            rid, pid = topo.addr(h, core)
+            a, b = piece(2 * i + j)
+            eng = topo.engines(core, h)[j::2]
+            trs.append(RemoteDMATransfer(dst_ids=[DstId(rid=rid, pnc=pid)], dma_engine_mask=sum(1 << e for e in eng),
+                                         remote_sem=T.sem["hp%d" % (i // 2)], src=T.taba[:, a:b], dst=T.taba[:, a:b]))
+            cnt["sent"] += len(eng)
+        g.remote_dma_fused(trs, local_sem=T.sem.sent)
+    hp = helpers_of(prev, core, T, topo)
+    for lay in range(2):
+        cnt["arr%d" % lay] = sum(len(topo.engines(hp[i % len(hp)], core)) for i in range(4 * lay, 4 * lay + 4))
+    for name in ("am1", "am2", "ap0", "ap1"):
+        cnt[name] = len(topo.engines(partner, core))
+    prid, ppid = topo.addr(partner, core)
+
+    def to_partner(dst, src, ready, arrive):
+        wait(g, ready)
+        g.remote_dma(dst, src, T.sem[arrive], T.sem.sent, ppid, prid, topo.mask(core, partner))
+        cnt["sent"] += len(topo.engines(core, partner))
+
+    def pos(k):
+        return T.pos[:, 128 * k:128 * (k + 1)]
+
+    def wf(k):
+        return T.wf[:, 128 * k:128 * (k + 1)]
+
+    where = [(T.taba, 0, ("ld0", "ld1")), (T.taba, 1, ("ld2", "ld3")), (T.tabb, 0, ("arr0",)), (T.tabb, 1, ("arr1",)),
+             (T.taba, 0, ()), (T.taba, 1, ()), (T.tabb, 0, ()), (T.tabb, 1, ())]
+
+    def gather(k, offs, ready):
+        tab, l, need = where[k]
+        win = tab[:, (SEL + CELLS) * l:(SEL + CELLS) * l + CELLS]
+        o = R * k
+        wait(S, ready, *need)
+        inc(S.activation(T.gat[:, o:o + 16 * SPLIT], win.indirect(offs(0, SPLIT)), ActivationFunctionType.Copy), "gs")
+        wait(V, ready, *need)
+        inc(V.tensor_copy(T.gat[:, o + 16 * SPLIT:o + R], win.indirect(offs(SPLIT, NL))), "gv")
+
+    def slopes(k):
+        tab, l, need = where[k]
+        wait(PE, "gs", "gv")
+        for ch in range(8):
+            inc(PE.matmul(T.ps1[:, ch:128:8], T.gat[:, R * k + ch:R * (k + 1):8],
+                          tab[:, CELLS + 16 * l:CELLS + 16 * l + 16], True, True), "pe1")
+
+    def move(k):
+        wait(V, "v", "pe1")
+        inc(V.tensor_tensor(pos(k + 1), T.ps1[:, 0:128], wf(k), A.add), "v")
+
+    def cells(k):
+        o = 128 * k
+        wait(V, "v")
+        inc(ts(T.msk[:, 0:64], T.pos[:, o:o + 64], 4, A.arith_shift_right, 63, A.bitwise_and), "v")
+        inc(ts(T.msk[:, 64:128], T.pos[:, o + 64:o + 128], 0x1F0, A.bitwise_and), "v")
+        wait(V, "v")
+        inc(V.tensor_copy(T.cv[:, 1::2, :], T.msk[:, :]), "cvt")
+        wait(PE, "cvt")
+        for j in range(4):
+            uv, h = j // 2, j % 2
+            b = 16 * uv + 1 - h
+            inc(PE.matmul(T.ps2[:, 0:64], T.cv[:, b:b + 16, :], T.rr[:, 64 * j:64 * j + 64], j == 0, j == 3), "pe2")
+
+    def offsets(out, name):
+        wait(V, "pe2")
+        inc(V.tensor_copy(out, T.ps2[:, 0:64]), name)
+
+    def twice(k):
+        inc(ts(T.tw[:, :], pos(k), 2.0, A.mult, -HALF, A.add), "v")
+
+    def ahead(k, old):
+        wait(V, "v")
+        inc(V.tensor_tensor(wf(k), T.tw[:, :], old, A.subtract), "v")
+
+    def sums(k, banks, start, stop, names=None):
+        for b in range(2):
+            ins = PE.matmul(banks[b][:, :], T.idb[:, :], T.gat[:, R * k + 512 * b:R * k + 512 * (b + 1)], start, stop)
+            if names:
+                inc(ins, names[b])
+
+    def own(k):
+        return lambda a, b: T.idx[:, NL * k + a:NL * k + b]
+
+    sa, sc = (T.sa0, T.sa1), (T.sc0, T.sc1)
+
+    wait(V, "pei")
+    inc(ts(pos(0), T.psi[:, 0:128], float(BIAS), A.add), "v")
+    cells(0)
+    inc(ts(wf(0), T.psi[:, 128:256], BIAS - HALF, A.add), "v")
+    offsets(T.idx[:, 0:NL], "idxr")
+    gather(0, own(0), "idxr")
+    inc(ts(T.idh[:, :], T.iot[:, 144:272], 0.0, A.is_equal), "cst")
+    wait(PE, "selr", "cst")
+    slopes(0)
+    move(0)
+    cells(1)
+    twice(1)
+    offsets(T.idx[:, NL:2 * NL], "idxr")
+    sums(0, sa, True, False)
+    gather(1, own(1), "idxr")
+    ahead(1, pos(0))
+    inc(V.tensor_copy(T.mo1[:, 128:256], pos(1)), "m1r")
+    slopes(1)
+    move(1)
+    sums(1, sa, False, False)
+    wait(V, "v")
+    inc(V.tensor_copy(T.mo1[:, 0:128], T.pos[:, 256:384]), "m1r")
+    to_partner(T.mi1[:, :], T.mo1[:, :], "m1r", "am1")
+
+    wait(V, "am1", "m1r")
+    inc(V.tensor_copy(pos(8), T.mi1[:, 0:128]), "v")
+    cells(8)
+    inc(V.tensor_copy(pos(9), T.mi1[:, 128:256]), "v")
+    twice(8)
+    offsets(T.idx[:, 2 * NL:3 * NL], "idxr")
+    old = pos(9)
+    for k in range(2, 6):
+        gather(k, own(k), "idxr")
+        ahead(k, old)
+        old = pos(8 if k == 2 else k)
+        slopes(k)
+        move(k)
+        cells(k + 1)
+        twice(k + 1)
+        sums(k, sc, k == 2, k == 5, ("c0", "c1") if k == 5 else None)
+        if k < 5:
+            offsets(T.idx[:, (k + 1) * NL:(k + 2) * NL], "idxr")
+    ahead(6, old)
+    wait(V, "v")
+    inc(V.tensor_copy(T.mo2[:, 64:192], wf(6)), "m2r")
+    offsets(T.mo2[:, 0:64], "m2r")
+    to_partner(T.mi2[:, :], T.mo2[:, :], "m2r", "am2")
+    for b in range(2):
+        wait(V, "c%d" % b)
+        inc(V.tensor_copy(T.pout[:, 512 * b:512 * (b + 1)], sc[b][:, :]), "pr%d" % b)
+        to_partner(T.pin[:, 512 * b:512 * (b + 1)], T.pout[:, 512 * b:512 * (b + 1)], "pr%d" % b, "ap%d" % b)
+
+    gather(6, lambda a, b: T.mi2[:, a:b], "am2")
+    wait(V, "m2r")
+    inc(ts(wf(6), T.mi2[:, 64:192], -HALF, A.add), "v")
+    slopes(6)
+    move(6)
+    cells(7)
+    offsets(T.idx[:, 7 * NL:8 * NL], "idxr")
+    sums(6, sa, False, False)
+    gather(7, own(7), "idxr")
+    for b in range(2):
+        wait(PE, "ap%d" % b)
+        PE.matmul(sa[b][:, :], T.idh[:, :], T.pin[:, 512 * b:512 * (b + 1)], False, False)
+    wait(PE, "gs", "gv")
+    sums(7, sa, False, True, ("a0", "a1"))
+    wait(S, "a0")
+    inc(S.activation(T.res[:, 0:512], T.sa0[:, :], ActivationFunctionType.Copy), "cp0")
+    wait(V, "a1")
+    inc(V.tensor_copy(T.res[:, 512:1024], T.sa1[:, :]), "cp1")
+    wait(S, "cp0")
+    inc(S.dma_start(T.y[:, 0:512], T.res[:, 0:512]), "st0", 16)
+    wait(SY, "cp1")
+    inc(SY.dma_start(T.y[:, 512:1024], T.res[:, 512:1024]), "st1", 16)
+    wait(g, "sent", "st0", "st1")

@@ -5,9 +5,15 @@ R, NL = 1024, 64
 CELLS = 2048
 SEL = 32
 TAB = SEL + 2 * CELLS
-BIAS = 1024
 HALF = 127.0 / 256.0
+SPLIT0 = 40
 SPLIT = 32
+WHOLE = 2.0 ** 23 + 2048
+CELL0 = 2560.0
+WRAPX0 = 196608.0
+WRAPY0 = 98304.0
+WEIGHTS = (1.0 / 16, 4.0, -1.0 / 16, -4.0)
+ORIGIN = -(CELL0 / 16 + 4 * CELL0 - WRAPX0 / 16 - 4 * WRAPY0)
 
 SCRATCH = {
     "taba": ("sbuf", [128, TAB], "bfloat16"),
@@ -16,49 +22,48 @@ SCRATCH = {
     "rays": ("sbuf", [128, 4 * NL], "int32"),
     "faci": ("sbuf", [128, 4], "int32"),
     "facf": ("sbuf", [128, 4], "float32"),
-    "iot": ("sbuf", [128, 272], "float32"),
+    "iot": ("sbuf", [128, 192], "float32"),
     "selb": ("sbuf", [128, 16], "float32"),
     "e01": ("sbuf", [128, 128], "float32"),
-    "e2": ("sbuf", [128, 64], "float32"),
     "mk": ("sbuf", [128, 4], "float32"),
-    "eh": ("sbuf", [128, 64], "float16"),
-    "rr": ("sbuf", [128, 256], "bfloat16"),
+    "eh": ("sbuf", [128, 128], "float16"),
+    "rr": ("sbuf", [128, 512], "bfloat16"),
     "idb": ("sbuf", [128, 128], "bfloat16"),
-    "idh": ("sbuf", [128, 128], "float16"),
+    "idh": ("sbuf", [128, 384], "float16"),
+    "hc": ("sbuf", [128, 128], "bfloat16"),
     "lt": ("sbuf", [128, 512], "float16"),
+    "c0y": ("sbuf", [128, NL], "bfloat16"),
+    "c0x": ("sbuf", [128, NL], "float32"),
+    "c0i": ("sbuf", [128, NL], "int32"),
     "idx": ("sbuf", [128, 8 * NL], "uint16"),
-    "pos": ("sbuf", [128, 10 * 128], "int32"),
-    "wf": ("sbuf", [128, 8 * 128], "float32"),
-    "tw": ("sbuf", [128, 128], "float32"),
-    "msk": ("sbuf", [128, 128], "int32"),
-    "cv": ("sbuf", [128, 33, 8], "bfloat16"),
-    "mo1": ("sbuf", [128, 256], "uint16"),
-    "mi1": ("sbuf", [128, 256], "uint16"),
-    "mo2": ("sbuf", [128, 192], "uint16"),
-    "mi2": ("sbuf", [128, 192], "uint16"),
+    "pos": ("sbuf", [128, 4 * 128], "float16"),
+    "cv": ("sbuf", [128, 65, 8], "bfloat16"),
+    "mo1": ("sbuf", [128, 256], "float16"),
+    "mi1": ("sbuf", [128, 256], "float16"),
+    "mo2": ("sbuf", [128, NL], "uint16"),
+    "mi2": ("sbuf", [128, NL], "uint16"),
+    "mo3": ("sbuf", [128, 128], "float16"),
+    "mi3": ("sbuf", [128, 128], "float16"),
     "pout": ("sbuf", [128, R], "float16"),
     "pin": ("sbuf", [128, R], "float16"),
     "res": ("sbuf", [128, R], "float32"),
     "sa0": ("psum", [128, 512], "float32"),
     "sa1": ("psum", [128, 512], "float32"),
+    "sa2": ("psum", [128, 512], "float32"),
+    "sa3": ("psum", [128, 512], "float32"),
     "sc0": ("psum", [128, 512], "float32"),
     "sc1": ("psum", [128, 512], "float32"),
     "ps1": ("psum", [128, 512], "float32"),
     "ps2": ("psum", [128, 512], "float32"),
-    "psi": ("psum", [128, 512], "float32"),
 }
-SEMAPHORES = ["ld0", "ld1", "ld2", "ld3", "ldf", "ldp", "fz", "io0", "io1", "io2", "io3", "v", "selr", "cst", "ltr",
-              "pei", "idxr", "gs", "gv", "pe1", "cvt", "pe2", "m1r", "m2r", "pr0", "pr1", "c0", "c1", "a0", "a1",
-              "arr0", "arr1", "am1", "am2", "ap0", "ap1", "sent", "hp0", "hp1", "cp0", "cp1", "st0", "st1"]
+SEMAPHORES = ["ld0", "ld1", "ld2", "ld3", "ldf", "ldp", "ldd", "io0", "io1", "v", "selr", "cst", "idr", "rrr", "lt0",
+              "lt1", "fz", "g0", "g1", "g2", "g3",
+              "idxr", "gs", "gv", "pe1", "cva", "cvb", "ex", "pe2", "pb", "m2r", "m3r", "pr0", "pr1", "c0", "c1",
+              "a0", "a1", "a2", "a3", "arr0", "arr1", "am1", "am2", "am3", "ap0", "ap1", "sent", "hp0", "hp1", "hp2",
+              "cpa", "cpb", "st0", "st1"]
 
 A = AluOpType
-
-
-def piece(i):
-    if i < 4:
-        w = (CELLS + SEL) // 4
-        return w * i, w * (i + 1)
-    return SEL + 512 * i, SEL + 512 * (i + 1)
+COPY = ActivationFunctionType.Copy
 
 
 def helpers_of(src, dst, T, topo):
@@ -71,6 +76,17 @@ def helpers_of(src, dst, T, topo):
     return out
 
 
+def rounds(nh):
+    w0, w1 = (CELLS + SEL) // (2 * nh), CELLS // nh
+    out = [[(j, w0 * (nh * i + j), w0 * (nh * i + j + 1)) for j in range(nh)] for i in range(2)]
+    o = CELLS + SEL
+    return out + [[(j, o + w1 * j, o + w1 * (j + 1)) for j in range(i * nh // 2, (i + 1) * nh // 2)] for i in range(2)]
+
+
+def carriers(src, helper, partner, i, topo):
+    return [e for e in topo.engines(src, helper) if i < 3 or e not in topo.engines(src, partner)]
+
+
 def helper_program(g, core, T, topo):
     n = len(T.cores)
     for q in range(n):
@@ -79,17 +95,15 @@ def helper_program(g, core, T, topo):
         if core not in hs:
             continue
         rid, pid = topo.addr(dst, core)
-        ne_in, ne_out = len(topo.engines(src, core)) // 2, len(topo.engines(core, dst))
-        got, sent = [0, 0], 0
-        for i in range(8):
-            if hs[i % len(hs)] != core:
-                continue
-            lay = i // 4
-            a, b = piece(i)
-            got[lay] += ne_in
-            g.wait_ge(T.sem["hp%d" % lay], got[lay])
-            g.remote_dma(T.tabb[:, a:b], T.taba[:, a:b], T.sem["arr%d" % lay], T.sem.sent, pid, rid, topo.mask(core, dst))
-            sent += ne_out
+        sent = 0
+        for i, call in enumerate(rounds(len(hs))):
+            for j, a, b in call:
+                if hs[j] != core:
+                    continue
+                g.wait_ge(T.sem["hp%d" % min(i, 2)], len(carriers(src, core, T.cores[(q + 2) % n], i, topo)) // len(call))
+                g.remote_dma(T.tabb[:, a:b], T.taba[:, a:b], T.sem["arr%d" % (i // 2)], T.sem.sent, pid, rid,
+                             topo.mask(core, dst))
+                sent += len(topo.engines(core, dst))
         g.wait_ge(T.sem.sent, sent)
 
 
@@ -116,84 +130,87 @@ def rank_program(g, core, T, topo):
             return V.tensor_scalar(out, in0, s1, None, op0)
         return V.tensor_scalar(out, in0, s1, s2, op0, op1)
 
+    hs = helpers_of(core, nxt, T, topo)
+    calls = rounds(len(hs))
+
     def load_tab(q, i):
-        a, b = piece(2 * i)[0], min(piece(2 * i + 1)[1], CELLS if i < 2 else TAB)
+        a, b = calls[i][0][1], min(calls[i][-1][2], CELLS if i < 2 else TAB)
         o = 0 if i < 2 else SEL
         inc(q.dma_start(T.taba[:, a:b], T.lay[:, a - o:b - o]), "ld%d" % i, 16)
     inc(V.memset(T.faci[:, :], 0), "fz")
     load_tab(SY, 0)
-    inc(S.dma_start(T.rays[64:96, :], T.dx[:, :]), "ldp", 16)
-    inc(SY.dma_start(T.rays[0:32, :], T.px[:, :]), "ldp", 16)
-    inc(S.dma_start(T.rays[96:128, :], T.dy[:, :]), "ldp", 16)
-    inc(SY.dma_start(T.rays[32:64, :], T.py[:, :]), "ldp", 16)
+    inc(S.dma_start(T.rays[:, 0:NL], T.px[:, :]), "ldp", 16)
+    inc(S.dma_start(T.rays[:, NL:2 * NL], T.py[:, :]), "ldp", 16)
+    load_tab(SY, 1)
     wait(S, "fz")
     for uv in range(2):
         inc(S.dma_start(T.faci[14 + uv::16, 0:2], T.fac[14 + uv::16, :]), "ldf", 16)
-    load_tab(SY, 1)
-    load_tab(S, 2)
-    load_tab(SY, 3)
+    inc(SY.dma_start(T.rays[:, 2 * NL:3 * NL], T.dx[:, :]), "ldd", 16)
+    inc(S.dma_start(T.rays[:, 3 * NL:4 * NL], T.dy[:, :]), "ldd", 16)
+    load_tab(SY, 2)
+    load_tab(S, 3)
 
-    def iota(out, pattern, base, cm, name):
-        inc(g.iota(out, pattern, base, cm, allow_small_or_imprecise_dtypes=True), name)
-    iota(T.iot[:, 16:80], [[-1, 2], [-32, 4], [-4, 8]], 0, 1, "io1")
-    iota(T.iot[:, 0:16], [[1, 2], [16, 8]], 14, -1, "io0")
-    iota(T.iot[:, 80:144], [[-2, 64]], 0, 1, "io2")
-    iota(T.iot[:, 144:272], [[-1, 128]], 0, 1, "io3")
-    inc(V.memset(T.cv[:, :, :], 0.0), "v")
+    def iota(out, pattern, name):
+        inc(g.iota(out, pattern, 0, 1, allow_small_or_imprecise_dtypes=True), name)
+    iota(T.iot[:, 0:128], [[-1, 128]], "io0")
+    iota(T.iot[:, 128:192], [[-16, 8], [-1, 8]], "io1")
+    inc(V.memset(T.cv[:, :, :], 0.0), "cst")
+    inc(V.memset(T.hc[:, :], -HALF), "cst")
+    wait(V, "io0")
+    inc(ts(T.idb[:, :], T.iot[:, 0:128], 0.0, A.is_equal), "idr")
+    for uv in range(2):
+        inc(ts(T.selb[:, 8 * uv:8 * uv + 8], T.iot[:, 14 + uv:128:16], 0.0, A.is_equal, 1.0 / 128.0, A.mult), "v")
     wait(V, "io1")
     for h in range(2):
-        inc(ts(T.e01[:, 64 * h:64 * h + 64], T.iot[:, 16:80], 2.0 * h, A.is_equal), "v")
-    wait(V, "io0")
-    inc(ts(T.selb[:, :], T.iot[:, 0:16], 0.0, A.is_equal, 1.0 / 128.0, A.mult), "v")
-    wait(V, "v")
+        inc(ts(T.e01[:, 64 * h:64 * h + 64], T.iot[:, 128:192], 8.0 * h, A.is_equal), "v")
+    wait(V, "v", "idr")
     for h in range(2):
         inc(V.tensor_reduce(T.mk[:, h:h + 1], T.e01[:, 64 * h:64 * h + 64], AxisListType.X, A.add), "v")
-    inc(V.tensor_tensor(T.e2[:, :], T.e01[:, 0:64], T.e01[:, 64:128], A.add), "v")
+    inc(V.tensor_tensor(T.eh[:, 0:64], T.e01[:, 0:64], T.e01[:, 64:128], A.add), "v")
+    for j, w in enumerate((2.0, -1.0, 1.0)):
+        inc(ts(T.idh[:, 128 * j:128 * j + 128], T.idb[:, :], w, A.mult), "cst")
     wait(V, "v")
-    for c2 in range(2):
-        o = 32 * c2
-        inc(V.tensor_copy(T.eh[:, o:o + 16], T.e2[:, o:o + 16]), "cst")
-        inc(V.tensor_tensor(T.eh[:, o + 16:o + 32], T.e2[:, o:o + 16], T.e2[:, o + 16:o + 32], A.add), "cst")
-    wait(V, "io2")
-    for uv in range(2):
-        for h in range(2):
-            c = 128 * uv + 64 * h
-            inc(ts(T.rr[:, c:c + 64], T.iot[:, 80:144], float(h), A.is_equal, 4.0 if uv else 1.0, A.mult), "cst")
+    inc(ts(T.eh[:, 64:128], T.eh[:, 0:64], -1.0, A.mult), "cst")
+    wait(S, "idr")
+    for j, w in enumerate(WEIGHTS):
+        inc(S.activation(T.rr[:, 128 * j:128 * j + 128], T.idb[:, :], COPY, scale=w), "rrr")
+    two, minus, one = (T.idh[:, 128 * j:128 * j + 128] for j in range(3))
+
     wait(V, "ldp")
-    for h in range(2):
-        inc(ts(T.lt[:, h::2], T.rays[:, :], T.mk[:, h:h + 1], A.mult), "ltr")
-    wait(PE, "cst", "ltr")
-    for ch in range(8):
-        c2, c4 = ch // 4, ch % 4
-        inc(PE.matmul(T.psi[:, ch:256:8], T.lt[:, 128 * c4:128 * c4 + 128], T.eh[:, 32 * c2:32 * c2 + 32], True, True), "pei")
+    inc(ts(T.c0y[:, :], T.rays[:, NL:2 * NL], 4.0, A.mult, 12288.0 - 30.0, A.add), "v")
+    inc(ts(T.c0x[:, :], T.rays[:, 0:NL], 1.0 / 16, A.mult, -12288.0 - 15.0 / 32, A.add), "v")
+    wait(V, "v")
+    inc(V.tensor_tensor(T.c0i[:, :], T.c0x[:, :], T.c0y[:, :], A.add), "v")
     wait(V, "ldf")
     inc(V.tensor_copy(T.facf[:, 0:2], T.faci[:, 0:2]), "v")
-    wait(V, "io3")
-    inc(ts(T.idb[:, :], T.iot[:, 144:272], 0.0, A.is_equal), "cst")
     wait(V, "v")
+    inc(V.tensor_copy(T.idx[:, 0:NL], T.c0i[:, :]), "idxr")
     for l in range(2):
         inc(ts(T.taba[:, CELLS + 16 * l:CELLS + 16 * l + 16], T.selb[:, :], T.facf[:, l:l + 1], A.mult), "selr")
 
-    hs = helpers_of(core, nxt, T, topo)
+    def halves(j):
+        for h in range(2):
+            inc(ts(T.lt[:, 256 * j + h:256 * j + 256:2], T.rays[:, 128 * j:128 * j + 128], T.mk[:, h:h + 1], A.mult),
+                "lt%d" % j)
+    halves(0)
+
     cnt["sent"] = 0
-    for i in range(4):
+    for i, call in enumerate(calls):
         wait(g, "ld%d" % i)
         if i == 1:
             wait(g, "selr")
         trs = []
-        for j in range(2):
-            h = hs[(2 * i + j) % len(hs)]
-            rid, pid = topo.addr(h, core)
-            a, b = piece(2 * i + j)
-            eng = topo.engines(core, h)[j::2]
+        for j, (k, a, b) in enumerate(call):
+            rid, pid = topo.addr(hs[k], core)
+            eng = carriers(core, hs[k], partner, i, topo)[j::len(call)]
             trs.append(RemoteDMATransfer(dst_ids=[DstId(rid=rid, pnc=pid)], dma_engine_mask=sum(1 << e for e in eng),
-                                         remote_sem=T.sem["hp%d" % (i // 2)], src=T.taba[:, a:b], dst=T.taba[:, a:b]))
+                                         remote_sem=T.sem["hp%d" % min(i, 2)], src=T.taba[:, a:b], dst=T.taba[:, a:b]))
             cnt["sent"] += len(eng)
         g.remote_dma_fused(trs, local_sem=T.sem.sent)
     hp = helpers_of(prev, core, T, topo)
     for lay in range(2):
-        cnt["arr%d" % lay] = sum(len(topo.engines(hp[i % len(hp)], core)) for i in range(4 * lay, 4 * lay + 4))
-    for name in ("am1", "am2", "ap0", "ap1"):
+        cnt["arr%d" % lay] = sum(len(topo.engines(hp[k], core)) for call in calls[2 * lay:2 * lay + 2] for k, a, b in call)
+    for name in ("am1", "am2", "am3", "ap0", "ap1"):
         cnt[name] = len(topo.engines(partner, core))
     prid, ppid = topo.addr(partner, core)
 
@@ -202,142 +219,160 @@ def rank_program(g, core, T, topo):
         g.remote_dma(dst, src, T.sem[arrive], T.sem.sent, ppid, prid, topo.mask(core, partner))
         cnt["sent"] += len(topo.engines(core, partner))
 
-    def pos(k):
-        return T.pos[:, 128 * k:128 * (k + 1)]
-
-    def wf(k):
-        return T.wf[:, 128 * k:128 * (k + 1)]
-
     where = [(T.taba, 0, ("ld0", "ld1")), (T.taba, 1, ("ld2", "ld3")), (T.tabb, 0, ("arr0",)), (T.tabb, 1, ("arr1",)),
              (T.taba, 0, ()), (T.taba, 1, ()), (T.tabb, 0, ()), (T.tabb, 1, ())]
+    Z = T.ps1[:, 0:128]
 
-    def gather(k, offs, ready):
+    def window(k):
         tab, l, need = where[k]
-        win = tab[:, (SEL + CELLS) * l:(SEL + CELLS) * l + CELLS]
-        o = R * k
-        wait(S, ready, *need)
-        inc(S.activation(T.gat[:, o:o + 16 * SPLIT], win.indirect(offs(0, SPLIT)), ActivationFunctionType.Copy), "gs")
-        wait(V, ready, *need)
-        inc(V.tensor_copy(T.gat[:, o + 16 * SPLIT:o + R], win.indirect(offs(SPLIT, NL))), "gv")
+        return tab[:, (SEL + CELLS) * l:(SEL + CELLS) * l + CELLS]
+
+    def idx(k, a=0, b=NL):
+        return T.mi2[:, a:b] if k == 6 else T.idx[:, NL * k + a:NL * k + b]
+
+    def gat(k, a, b):
+        return T.gat[:, R * k + a:R * k + b]
+
+    def gather(k, ready="idxr", split=SPLIT):
+        wait(S, ready, *where[k][2])
+        inc(S.activation(gat(k, 0, 16 * split), window(k).indirect(idx(k, 0, split)), COPY), "gs")
+        wait(V, ready, *where[k][2])
+        inc(V.tensor_copy(gat(k, 16 * split, R), window(k).indirect(idx(k, split, NL))), "gv")
+
+    def base(terms, half=True, close=False):
+        if half:
+            terms = [(T.idb[:, :], T.hc[:, :])] + terms
+        for j, (w, x) in enumerate(terms):
+            ins = PE.matmul(Z, w, x, j == 0, close and j == len(terms) - 1)
+        inc(ins, "pb")
+
+    def turned(lists, sign):
+        wait(PE, "pb")
+        for j in lists:
+            inc(PE.matmul(T.ps1[:, 64 * (j % 2):64 * (j % 2) + 64], T.lt[:, 128 * j:128 * j + 128],
+                          T.eh[:, 64 * sign:64 * sign + 64], False, False), "pb")
 
     def slopes(k):
         tab, l, need = where[k]
-        wait(PE, "gs", "gv")
+        wait(PE, "pb", "gs", "gv")
         for ch in range(8):
             inc(PE.matmul(T.ps1[:, ch:128:8], T.gat[:, R * k + ch:R * (k + 1):8],
-                          tab[:, CELLS + 16 * l:CELLS + 16 * l + 16], True, True), "pe1")
+                          tab[:, CELLS + 16 * l:CELLS + 16 * l + 16], False, ch == 7), "pe1")
 
-    def move(k):
-        wait(V, "v", "pe1")
-        inc(V.tensor_tensor(pos(k + 1), T.ps1[:, 0:128], wf(k), A.add), "v")
+    def cells(z):
+        inc(ts(T.cv[:, 1:33:2, :], z[:, 0:128], CELL0 - 7.5, A.add), "cva")
+        inc(ts(T.cv[:, 33:49:2, :], z[:, 0:64], WHOLE, A.add, WHOLE - (WRAPX0 - 511.5), A.subtract), "cvb")
+        inc(ts(T.cv[:, 49:65:2, :], z[:, 64:128], WHOLE, A.add, WHOLE - (WRAPY0 - 255.5), A.subtract), "cvb")
+        for j in range(8):
+            c, h = j // 2, j % 2
+            if j % 4 == 0:
+                wait(PE, "cvb" if j else "cva")
+            b = 16 * c + 1 - h
+            ins = PE.matmul(T.ps2[:, 0:64], T.cv[:, b:b + 16, :], T.rr[:, 128 * c + h:128 * c + 128:2], j == 0, j == 7)
+        inc(ins, "pe2")
 
-    def cells(k):
-        o = 128 * k
-        wait(V, "v")
-        inc(ts(T.msk[:, 0:64], T.pos[:, o:o + 64], 4, A.arith_shift_right, 63, A.bitwise_and), "v")
-        inc(ts(T.msk[:, 64:128], T.pos[:, o + 64:o + 128], 0x1F0, A.bitwise_and), "v")
-        wait(V, "v")
-        inc(V.tensor_copy(T.cv[:, 1::2, :], T.msk[:, :]), "cvt")
-        wait(PE, "cvt")
-        for j in range(4):
-            uv, h = j // 2, j % 2
-            b = 16 * uv + 1 - h
-            inc(PE.matmul(T.ps2[:, 0:64], T.cv[:, b:b + 16, :], T.rr[:, 64 * j:64 * j + 64], j == 0, j == 3), "pe2")
+    def whole(out):
+        inc(ts(out, Z, WHOLE, A.add, WHOLE, A.subtract), "ex")
 
     def offsets(out, name):
         wait(V, "pe2")
-        inc(V.tensor_copy(out, T.ps2[:, 0:64]), name)
-
-    def twice(k):
-        inc(ts(T.tw[:, :], pos(k), 2.0, A.mult, -HALF, A.add), "v")
-
-    def ahead(k, old):
-        wait(V, "v")
-        inc(V.tensor_tensor(wf(k), T.tw[:, :], old, A.subtract), "v")
+        inc(ts(out, T.ps2[:, 0:64], ORIGIN, A.add), name)
 
     def sums(k, banks, start, stop, names=None):
-        for b in range(2):
-            ins = PE.matmul(banks[b][:, :], T.idb[:, :], T.gat[:, R * k + 512 * b:R * k + 512 * (b + 1)], start, stop)
+        w = R // len(banks)
+        for b, bank in enumerate(banks):
+            ins = PE.matmul(bank[:, 0:w], T.idb[:, :], gat(k, w * b, w * (b + 1)), start, stop)
             if names:
                 inc(ins, names[b])
 
-    def own(k):
-        return lambda a, b: T.idx[:, NL * k + a:NL * k + b]
+    sa, sc = (T.sa0, T.sa1, T.sa2, T.sa3), (T.sc0, T.sc1)
+    p1, p2 = T.mo1[:, 128:256], T.mo1[:, 0:128]
 
-    sa, sc = (T.sa0, T.sa1), (T.sc0, T.sc1)
-
-    wait(V, "pei")
-    inc(ts(pos(0), T.psi[:, 0:128], float(BIAS), A.add), "v")
-    cells(0)
-    inc(ts(wf(0), T.psi[:, 128:256], BIAS - HALF, A.add), "v")
-    offsets(T.idx[:, 0:NL], "idxr")
-    gather(0, own(0), "idxr")
-    inc(ts(T.idh[:, :], T.iot[:, 144:272], 0.0, A.is_equal), "cst")
-    wait(PE, "selr", "cst")
+    wait(PE, "cst", "idr", "lt0")
+    base([])
+    turned((0, 1), 0)
+    gather(0, split=SPLIT0)
+    wait(V, "ldd")
+    halves(1)
+    wait(PE, "lt1")
+    turned((2, 3), 0)
+    wait(PE, "selr", "rrr")
     slopes(0)
-    move(0)
-    cells(1)
-    twice(1)
-    offsets(T.idx[:, NL:2 * NL], "idxr")
+    wait(V, "pe1")
+    cells(T.ps1)
+    whole(p1)
+    offsets(idx(1), "idxr")
+    wait(PE, "ex")
+    base([(two, p1)])
+    turned((0, 1), 1)
     sums(0, sa, True, False)
-    gather(1, own(1), "idxr")
-    ahead(1, pos(0))
-    inc(V.tensor_copy(T.mo1[:, 128:256], pos(1)), "m1r")
+    gather(1)
     slopes(1)
-    move(1)
+    wait(V, "pe1")
+    whole(p2)
+    to_partner(T.mi1[:, :], T.mo1[:, :], "ex", "am1")
     sums(1, sa, False, False)
-    wait(V, "v")
-    inc(V.tensor_copy(T.mo1[:, 0:128], T.pos[:, 256:384]), "m1r")
-    to_partner(T.mi1[:, :], T.mo1[:, :], "m1r", "am1")
 
-    wait(V, "am1", "m1r")
-    inc(V.tensor_copy(pos(8), T.mi1[:, 0:128]), "v")
-    cells(8)
-    inc(V.tensor_copy(pos(9), T.mi1[:, 128:256]), "v")
-    twice(8)
-    offsets(T.idx[:, 2 * NL:3 * NL], "idxr")
-    old = pos(9)
+    place = {1: T.mi1[:, 128:256], 2: T.mi1[:, 0:128]}
+    for k in range(3, 7):
+        place[k] = T.pos[:, 128 * (k - 3):128 * (k - 2)]
+    wait(V, "am1")
+    cells(T.mi1)
+    wait(PE, "ex", "am1")
     for k in range(2, 6):
-        gather(k, own(k), "idxr")
-        ahead(k, old)
-        old = pos(8 if k == 2 else k)
+        offsets(idx(k), "idxr")
+        base([(two, place[k]), (minus, place[k - 1])])
+        if k > 2:
+            sums(k - 1, sc, k == 3, False)
+        gather(k)
         slopes(k)
-        move(k)
-        cells(k + 1)
-        twice(k + 1)
-        sums(k, sc, k == 2, k == 5, ("c0", "c1") if k == 5 else None)
-        if k < 5:
-            offsets(T.idx[:, (k + 1) * NL:(k + 2) * NL], "idxr")
-    ahead(6, old)
-    wait(V, "v")
-    inc(V.tensor_copy(T.mo2[:, 64:192], wf(6)), "m2r")
-    offsets(T.mo2[:, 0:64], "m2r")
+        wait(V, "pe1")
+        cells(T.ps1)
+        whole(place[k + 1])
+        wait(PE, "ex")
+    offsets(T.mo2[:, :], "m2r")
     to_partner(T.mi2[:, :], T.mo2[:, :], "m2r", "am2")
+    base([(two, place[6]), (minus, place[5])], half=False, close=True)
+    sums(5, sc, False, True, ("c0", "c1"))
+    wait(V, "pb")
+    inc(V.tensor_copy(T.mo3[:, :], Z), "m3r")
+    to_partner(T.mi3[:, :], T.mo3[:, :], "m3r", "am3")
     for b in range(2):
         wait(V, "c%d" % b)
         inc(V.tensor_copy(T.pout[:, 512 * b:512 * (b + 1)], sc[b][:, :]), "pr%d" % b)
         to_partner(T.pin[:, 512 * b:512 * (b + 1)], T.pout[:, 512 * b:512 * (b + 1)], "pr%d" % b, "ap%d" % b)
 
-    gather(6, lambda a, b: T.mi2[:, a:b], "am2")
-    wait(V, "m2r")
-    inc(ts(wf(6), T.mi2[:, 64:192], -HALF, A.add), "v")
+    gather(6, "am2")
+    wait(PE, "m2r", "m3r", "am3")
+    base([(one, T.mi3[:, :])])
     slopes(6)
-    move(6)
-    cells(7)
-    offsets(T.idx[:, 7 * NL:8 * NL], "idxr")
+    wait(V, "pe1")
+    cells(T.ps1)
+    offsets(idx(7), "idxr")
     sums(6, sa, False, False)
-    gather(7, own(7), "idxr")
-    for b in range(2):
-        wait(PE, "ap%d" % b)
-        PE.matmul(sa[b][:, :], T.idh[:, :], T.pin[:, 512 * b:512 * (b + 1)], False, False)
-    wait(PE, "gs", "gv")
-    sums(7, sa, False, True, ("a0", "a1"))
-    wait(S, "a0")
-    inc(S.activation(T.res[:, 0:512], T.sa0[:, :], ActivationFunctionType.Copy), "cp0")
-    wait(V, "a1")
-    inc(V.tensor_copy(T.res[:, 512:1024], T.sa1[:, :]), "cp1")
-    wait(S, "cp0")
-    inc(S.dma_start(T.y[:, 0:512], T.res[:, 0:512]), "st0", 16)
-    wait(SY, "cp1")
-    inc(SY.dma_start(T.y[:, 512:1024], T.res[:, 512:1024]), "st1", 16)
+    wait(S, "idxr")
+    wait(V, "idxr")
+    for b in range(4):
+        out, src = gat(7, 256 * b, 256 * (b + 1)), window(7).indirect(idx(7, 16 * b, 16 * (b + 1)))
+        if b % 2 == 0:
+            inc(S.activation(out, src, COPY), "g%d" % b)
+            wait(PE, "ap%d" % (b // 2))
+            for c in (b, b + 1):
+                PE.matmul(sa[c][:, 0:256], one, T.pin[:, 256 * c:256 * (c + 1)], False, False)
+        else:
+            inc(V.tensor_copy(out, src), "g%d" % b)
+        wait(PE, "g%d" % b)
+        inc(PE.matmul(sa[b][:, 0:256], T.idb[:, :], out, False, True), "a%d" % b)
+    for b in range(4):
+        out, name = T.res[:, 256 * b:256 * (b + 1)], "cpb" if b // 2 else "cpa"
+        if b % 2 == 0:
+            wait(S, "a%d" % b)
+            inc(S.activation(out, sa[b][:, 0:256], COPY), name)
+        else:
+            wait(V, "a%d" % b)
+            inc(V.tensor_copy(out, sa[b][:, 0:256]), name)
+    wait(SY, "cpa")
+    inc(SY.dma_start(T.y[:, 0:512], T.res[:, 0:512]), "st0", 16)
+    wait(S, "cpb")
+    inc(S.dma_start(T.y[:, 512:1024], T.res[:, 512:1024]), "st1", 16)
     wait(g, "sent", "st0", "st1")

@@ -5,9 +5,11 @@ R, NL = 1024, 64
 CELLS = 2048
 SEL = 32
 TAB = SEL + 2 * CELLS
+FIRST = 96
+LAST = 1120
 HALF = 127.0 / 256.0
-SPLIT0 = 40
 SPLIT = 32
+PARTS = (0, 256, 512, 736, R)
 WHOLE = 2.0 ** 23 + 2048
 CELL0 = 2560.0
 WRAPX0 = 196608.0
@@ -20,21 +22,21 @@ SCRATCH = {
     "tabb": ("sbuf", [128, TAB], "bfloat16"),
     "gat": ("sbuf", [128, 8 * R], "bfloat16"),
     "rays": ("sbuf", [128, 4 * NL], "int32"),
-    "faci": ("sbuf", [128, 4], "int32"),
-    "facf": ("sbuf", [128, 4], "float32"),
-    "iot": ("sbuf", [128, 192], "float32"),
+    "faci": ("sbuf", [128, 2], "int32"),
+    "facf": ("sbuf", [128, 2], "float32"),
+    "iot": ("sbuf", [128, 324], "float32"),
     "selb": ("sbuf", [128, 16], "float32"),
     "e01": ("sbuf", [128, 128], "float32"),
+    "e2": ("sbuf", [128, 2, 32], "float32"),
     "mk": ("sbuf", [128, 4], "float32"),
-    "eh": ("sbuf", [128, 128], "float16"),
+    "eh": ("sbuf", [128, 4, 16], "float16"),
+    "kk": ("sbuf", [128, 132], "bfloat16"),
+    "cel": ("sbuf", [128, 256], "bfloat16"),
     "rr": ("sbuf", [128, 512], "bfloat16"),
     "idb": ("sbuf", [128, 128], "bfloat16"),
     "idh": ("sbuf", [128, 384], "float16"),
     "hc": ("sbuf", [128, 128], "bfloat16"),
     "lt": ("sbuf", [128, 512], "float16"),
-    "c0y": ("sbuf", [128, NL], "bfloat16"),
-    "c0x": ("sbuf", [128, NL], "float32"),
-    "c0i": ("sbuf", [128, NL], "int32"),
     "idx": ("sbuf", [128, 8 * NL], "uint16"),
     "pos": ("sbuf", [128, 4 * 128], "float16"),
     "cv": ("sbuf", [128, 65, 8], "bfloat16"),
@@ -46,6 +48,7 @@ SCRATCH = {
     "mi3": ("sbuf", [128, 128], "float16"),
     "pout": ("sbuf", [128, R], "float16"),
     "pin": ("sbuf", [128, R], "float16"),
+    "pre": ("sbuf", [128, PARTS[1]], "float32"),
     "res": ("sbuf", [128, R], "float32"),
     "sa0": ("psum", [128, 512], "float32"),
     "sa1": ("psum", [128, 512], "float32"),
@@ -57,10 +60,10 @@ SCRATCH = {
     "ps2": ("psum", [128, 512], "float32"),
 }
 SEMAPHORES = ["ld0", "ld1", "ld2", "ld3", "ldf", "ldp", "ldd", "io0", "io1", "v", "selr", "cst", "idr", "rrr", "lt0",
-              "lt1", "fz", "g0", "g1", "g2", "g3",
-              "idxr", "gs", "gv", "pe1", "cva", "cvb", "ex", "pe2", "pb", "m2r", "m3r", "pr0", "pr1", "c0", "c1",
-              "a0", "a1", "a2", "a3", "arr0", "arr1", "am1", "am2", "am3", "ap0", "ap1", "sent", "hp0", "hp1", "hp2",
-              "cpa", "cpb", "st0", "st1"]
+              "idw", "io2", "fz", "g0", "g1", "g2", "g3",
+              "idxr", "gs", "gv", "pe1", "cv0", "cv1", "cv2", "cv3", "ex", "pe2", "pb", "m2r", "m3r", "pr0", "pr1", "c0", "c1",
+              "a0", "a1", "a2", "a3", "arr0", "arr1", "am0", "am1", "am2", "am3", "ap0", "ap1", "ap2", "pr2", "sent", "hp0", "hp1", "hp2", "hp3", "hp4",
+              "cp0", "cp1", "cp2", "cp3", "pre", "st"]
 
 A = AluOpType
 COPY = ActivationFunctionType.Copy
@@ -77,14 +80,17 @@ def helpers_of(src, dst, T, topo):
 
 
 def rounds(nh):
-    w0, w1 = (CELLS + SEL) // (2 * nh), CELLS // nh
-    out = [[(j, w0 * (nh * i + j), w0 * (nh * i + j + 1)) for j in range(nh)] for i in range(2)]
     o = CELLS + SEL
-    return out + [[(j, o + w1 * j, o + w1 * (j + 1)) for j in range(i * nh // 2, (i + 1) * nh // 2)] for i in range(2)]
+    w0, m = (o - FIRST) // (2 * nh), nh // 2
+    out = [[(0, 0, FIRST)]]
+    out += [[(j, a + w0 * j, a + w0 * (j + 1)) for j in range(nh)] for a in (FIRST, FIRST + nh * w0)]
+    for i, (a, w) in enumerate(((o, (CELLS - LAST) // m), (TAB - LAST, LAST // m))):
+        out.append([(m * i + j, a + w * j, a + w * (j + 1)) for j in range(m)])
+    return out
 
 
 def carriers(src, helper, partner, i, topo):
-    return [e for e in topo.engines(src, helper) if i < 3 or e not in topo.engines(src, partner)]
+    return [e for e in topo.engines(src, helper) if i != 3 or e not in topo.engines(src, partner)]
 
 
 def helper_program(g, core, T, topo):
@@ -100,8 +106,8 @@ def helper_program(g, core, T, topo):
             for j, a, b in call:
                 if hs[j] != core:
                     continue
-                g.wait_ge(T.sem["hp%d" % min(i, 2)], len(carriers(src, core, T.cores[(q + 2) % n], i, topo)) // len(call))
-                g.remote_dma(T.tabb[:, a:b], T.taba[:, a:b], T.sem["arr%d" % (i // 2)], T.sem.sent, pid, rid,
+                g.wait_ge(T.sem["hp%d" % i], len(carriers(src, core, T.cores[(q + 2) % n], i, topo)) // len(call))
+                g.remote_dma(T.tabb[:, a:b], T.taba[:, a:b], T.sem["arr%d" % (i // 3)], T.sem.sent, pid, rid,
                              topo.mask(core, dst))
                 sent += len(topo.engines(core, dst))
         g.wait_ge(T.sem.sent, sent)
@@ -134,83 +140,87 @@ def rank_program(g, core, T, topo):
     calls = rounds(len(hs))
 
     def load_tab(q, i):
-        a, b = calls[i][0][1], min(calls[i][-1][2], CELLS if i < 2 else TAB)
-        o = 0 if i < 2 else SEL
-        inc(q.dma_start(T.taba[:, a:b], T.lay[:, a - o:b - o]), "ld%d" % i, 16)
+        a, b = calls[i][0][1], min(calls[i][-1][2], CELLS)
+        inc(q.dma_start(T.taba[:, a:b], T.lay[:, a:b]), "ld%d" % i, 16)
     inc(V.memset(T.faci[:, :], 0), "fz")
     load_tab(SY, 0)
-    inc(S.dma_start(T.rays[:, 0:NL], T.px[:, :]), "ldp", 16)
-    inc(S.dma_start(T.rays[:, NL:2 * NL], T.py[:, :]), "ldp", 16)
-    load_tab(SY, 1)
+    for v, src in enumerate((T.px, T.py, T.dx, T.dy)):
+        inc((S, SY)[v % 2].dma_start(T.rays[32 * v:32 * v + 32, :], src[:, :]), "ldd" if v // 2 else "ldp", 16)
     wait(S, "fz")
     for uv in range(2):
-        inc(S.dma_start(T.faci[14 + uv::16, 0:2], T.fac[14 + uv::16, :]), "ldf", 16)
-    inc(SY.dma_start(T.rays[:, 2 * NL:3 * NL], T.dx[:, :]), "ldd", 16)
-    inc(S.dma_start(T.rays[:, 3 * NL:4 * NL], T.dy[:, :]), "ldd", 16)
+        inc(S.dma_start(T.faci[14 + uv::16, :], T.fac[14 + uv::16, :]), "ldf", 16)
+    load_tab(SY, 1)
     load_tab(SY, 2)
-    load_tab(S, 3)
+    inc(SY.dma_start(T.taba[:, CELLS + SEL:TAB], T.lay[:, CELLS:2 * CELLS]), "ld3", 16)
 
-    def iota(out, pattern, name):
-        inc(g.iota(out, pattern, 0, 1, allow_small_or_imprecise_dtypes=True), name)
-    iota(T.iot[:, 0:128], [[-1, 128]], "io0")
-    iota(T.iot[:, 128:192], [[-16, 8], [-1, 8]], "io1")
+    def iota(out, pattern, step, name):
+        inc(g.iota(out, pattern, 0, step, allow_small_or_imprecise_dtypes=True), name)
+    iota(T.iot[0:64, 192:324], [[1, 132]], -4, "io2")
+    iota(T.iot[:, 128:192], [[-1, 2], [-32, 4], [-4, 8]], 1, "io1")
+    iota(T.iot[:, 0:128], [[-1, 128]], 1, "io0")
     inc(V.memset(T.cv[:, :, :], 0.0), "cst")
     inc(V.memset(T.hc[:, :], -HALF), "cst")
+    wait(V, "io2")
+    for v in range(2):
+        inc(ts(T.kk[32 * v:32 * v + 32, :], T.iot[32 * v:32 * v + 32, 192:324], 3.0 - 128 * v, A.is_equal, WEIGHTS[v],
+               A.mult), "cst")
+    wait(V, "io1")
+    for h in range(2):
+        inc(ts(T.e01[:, 64 * h:64 * h + 64], T.iot[:, 128:192], 2.0 * h, A.is_equal), "v")
+    wait(V, "v")
+    for h in range(2):
+        inc(V.tensor_reduce(T.mk[:, h:h + 1], T.e01[:, 64 * h:64 * h + 64], AxisListType.X, A.add), "v")
+    inc(V.tensor_tensor(T.e2[:, :, :], T.e01[:, 0:64], T.e01[:, 64:128], A.add), "v")
     wait(V, "io0")
     inc(ts(T.idb[:, :], T.iot[:, 0:128], 0.0, A.is_equal), "idr")
     for uv in range(2):
         inc(ts(T.selb[:, 8 * uv:8 * uv + 8], T.iot[:, 14 + uv:128:16], 0.0, A.is_equal, 1.0 / 128.0, A.mult), "v")
-    wait(V, "io1")
-    for h in range(2):
-        inc(ts(T.e01[:, 64 * h:64 * h + 64], T.iot[:, 128:192], 8.0 * h, A.is_equal), "v")
-    wait(V, "v", "idr")
-    for h in range(2):
-        inc(V.tensor_reduce(T.mk[:, h:h + 1], T.e01[:, 64 * h:64 * h + 64], AxisListType.X, A.add), "v")
-    inc(V.tensor_tensor(T.eh[:, 0:64], T.e01[:, 0:64], T.e01[:, 64:128], A.add), "v")
-    for j, w in enumerate((2.0, -1.0, 1.0)):
-        inc(ts(T.idh[:, 128 * j:128 * j + 128], T.idb[:, :], w, A.mult), "cst")
     wait(V, "v")
-    inc(ts(T.eh[:, 64:128], T.eh[:, 0:64], -1.0, A.mult), "cst")
+    inc(V.tensor_tensor(T.eh[:, 0:2, :], T.e2[:, :, 0:16], T.e2[:, :, 16:32], A.add), "cst")
+    inc(ts(T.eh[:, 2:4, :], T.e2[:, :, 0:16], -1.0, A.mult), "cst")
     wait(S, "idr")
     for j, w in enumerate(WEIGHTS):
         inc(S.activation(T.rr[:, 128 * j:128 * j + 128], T.idb[:, :], COPY, scale=w), "rrr")
     two, minus, one = (T.idh[:, 128 * j:128 * j + 128] for j in range(3))
 
     wait(V, "ldp")
-    inc(ts(T.c0y[:, :], T.rays[:, NL:2 * NL], 4.0, A.mult, 12288.0 - 30.0, A.add), "v")
-    inc(ts(T.c0x[:, :], T.rays[:, 0:NL], 1.0 / 16, A.mult, -12288.0 - 15.0 / 32, A.add), "v")
-    wait(V, "v")
-    inc(V.tensor_tensor(T.c0i[:, :], T.c0x[:, :], T.c0y[:, :], A.add), "v")
+    inc(ts(T.cel[0:64, :], T.rays[0:64, :], CELL0 - 7.5, A.add), "cv0")
+    wait(PE, "cst", "cv0")
+    for c4 in range(4):
+        ins = PE.matmul(T.ps2[:, 0:64], T.kk[0:64, 3 - c4:131 - c4], T.cel[0:64, 64 * c4:64 * c4 + 64], c4 == 0, c4 == 3)
+    inc(ins, "pe2")
+    wait(V, "ldd")
+    inc(ts(T.lt[:, 0::2], T.rays[:, :], T.mk[:, 0:1], A.mult), "lt0")
+    wait(V, "pe2")
+    inc(ts(T.idx[:, 0:NL], T.ps2[:, 0:64], -CELL0 * (WEIGHTS[0] + WEIGHTS[1]), A.add), "idxr")
+    inc(ts(T.lt[:, 1::2], T.rays[:, :], T.mk[:, 1:2], A.mult), "lt0")
     wait(V, "ldf")
-    inc(V.tensor_copy(T.facf[:, 0:2], T.faci[:, 0:2]), "v")
+    inc(V.tensor_copy(T.facf[:, :], T.faci[:, :]), "v")
     wait(V, "v")
-    inc(V.tensor_copy(T.idx[:, 0:NL], T.c0i[:, :]), "idxr")
     for l in range(2):
         inc(ts(T.taba[:, CELLS + 16 * l:CELLS + 16 * l + 16], T.selb[:, :], T.facf[:, l:l + 1], A.mult), "selr")
 
-    def halves(j):
-        for h in range(2):
-            inc(ts(T.lt[:, 256 * j + h:256 * j + 256:2], T.rays[:, 128 * j:128 * j + 128], T.mk[:, h:h + 1], A.mult),
-                "lt%d" % j)
-    halves(0)
-
     cnt["sent"] = 0
-    for i, call in enumerate(calls):
-        wait(g, "ld%d" % i)
-        if i == 1:
+
+    def to_helpers(i):
+        call = calls[i]
+        wait(g, "ld%d" % min(i, 3))
+        if i == 2:
             wait(g, "selr")
         trs = []
         for j, (k, a, b) in enumerate(call):
             rid, pid = topo.addr(hs[k], core)
             eng = carriers(core, hs[k], partner, i, topo)[j::len(call)]
             trs.append(RemoteDMATransfer(dst_ids=[DstId(rid=rid, pnc=pid)], dma_engine_mask=sum(1 << e for e in eng),
-                                         remote_sem=T.sem["hp%d" % min(i, 2)], src=T.taba[:, a:b], dst=T.taba[:, a:b]))
+                                         remote_sem=T.sem["hp%d" % i], src=T.taba[:, a:b], dst=T.taba[:, a:b]))
             cnt["sent"] += len(eng)
         g.remote_dma_fused(trs, local_sem=T.sem.sent)
+    for i in range(3):
+        to_helpers(i)
     hp = helpers_of(prev, core, T, topo)
     for lay in range(2):
-        cnt["arr%d" % lay] = sum(len(topo.engines(hp[k], core)) for call in calls[2 * lay:2 * lay + 2] for k, a, b in call)
-    for name in ("am1", "am2", "am3", "ap0", "ap1"):
+        cnt["arr%d" % lay] = sum(len(topo.engines(hp[k], core)) for call in calls[3 * lay:3 * lay + 3] for k, a, b in call)
+    for name in ("am0", "am1", "am2", "am3", "ap0", "ap1", "ap2"):
         cnt[name] = len(topo.engines(partner, core))
     prid, ppid = topo.addr(partner, core)
 
@@ -219,7 +229,7 @@ def rank_program(g, core, T, topo):
         g.remote_dma(dst, src, T.sem[arrive], T.sem.sent, ppid, prid, topo.mask(core, partner))
         cnt["sent"] += len(topo.engines(core, partner))
 
-    where = [(T.taba, 0, ("ld0", "ld1")), (T.taba, 1, ("ld2", "ld3")), (T.tabb, 0, ("arr0",)), (T.tabb, 1, ("arr1",)),
+    where = [(T.taba, 0, ("ld0", "ld1", "ld2")), (T.taba, 1, ("ld3",)), (T.tabb, 0, ("arr0",)), (T.tabb, 1, ("arr1",)),
              (T.taba, 0, ()), (T.taba, 1, ()), (T.tabb, 0, ()), (T.tabb, 1, ())]
     Z = T.ps1[:, 0:128]
 
@@ -234,10 +244,10 @@ def rank_program(g, core, T, topo):
         return T.gat[:, R * k + a:R * k + b]
 
     def gather(k, ready="idxr", split=SPLIT):
-        wait(S, ready, *where[k][2])
+        wait(S, *where[k][2], ready)
         inc(S.activation(gat(k, 0, 16 * split), window(k).indirect(idx(k, 0, split)), COPY), "gs")
-        wait(V, ready, *where[k][2])
-        inc(V.tensor_copy(gat(k, 16 * split, R), window(k).indirect(idx(k, split, NL))), "gv")
+        wait(V, *where[k][2], ready)
+        inc(V.tensor_copy(gat(k, 16 * split, R), window(k).indirect(idx(k, split, NL))), "gs")
 
     def base(terms, half=True, close=False):
         if half:
@@ -246,27 +256,28 @@ def rank_program(g, core, T, topo):
             ins = PE.matmul(Z, w, x, j == 0, close and j == len(terms) - 1)
         inc(ins, "pb")
 
-    def turned(lists, sign):
+    def turned(j):
         wait(PE, "pb")
-        for j in lists:
-            inc(PE.matmul(T.ps1[:, 64 * (j % 2):64 * (j % 2) + 64], T.lt[:, 128 * j:128 * j + 128],
-                          T.eh[:, 64 * sign:64 * sign + 64], False, False), "pb")
+        for ch in range(8):
+            inc(PE.matmul(T.ps1[:, ch:128:8], T.lt[:, 128 * (ch % 4):128 * (ch % 4) + 128], T.eh[:, 2 * j + ch // 4, :],
+                          False, False), "pb")
 
     def slopes(k):
         tab, l, need = where[k]
-        wait(PE, "pb", "gs", "gv")
+        wait(PE, "pb", "gs")
         for ch in range(8):
             inc(PE.matmul(T.ps1[:, ch:128:8], T.gat[:, R * k + ch:R * (k + 1):8],
                           tab[:, CELLS + 16 * l:CELLS + 16 * l + 16], False, ch == 7), "pe1")
 
     def cells(z):
-        inc(ts(T.cv[:, 1:33:2, :], z[:, 0:128], CELL0 - 7.5, A.add), "cva")
-        inc(ts(T.cv[:, 33:49:2, :], z[:, 0:64], WHOLE, A.add, WHOLE - (WRAPX0 - 511.5), A.subtract), "cvb")
-        inc(ts(T.cv[:, 49:65:2, :], z[:, 64:128], WHOLE, A.add, WHOLE - (WRAPY0 - 255.5), A.subtract), "cvb")
+        inc(ts(T.cv[:, 1:17:2, :], z[:, 0:64], CELL0 - 7.5, A.add), "cv0")
+        inc(ts(T.cv[:, 17:33:2, :], z[:, 64:128], CELL0 - 7.5, A.add), "cv1")
+        inc(ts(T.cv[:, 33:49:2, :], z[:, 0:64], WHOLE, A.add, WHOLE - (WRAPX0 - 511.5), A.subtract), "cv2")
+        inc(ts(T.cv[:, 49:65:2, :], z[:, 64:128], WHOLE, A.add, WHOLE - (WRAPY0 - 255.5), A.subtract), "cv3")
         for j in range(8):
             c, h = j // 2, j % 2
-            if j % 4 == 0:
-                wait(PE, "cvb" if j else "cva")
+            if h == 0:
+                wait(PE, "cv%d" % c)
             b = 16 * c + 1 - h
             ins = PE.matmul(T.ps2[:, 0:64], T.cv[:, b:b + 16, :], T.rr[:, 128 * c + h:128 * c + 128:2], j == 0, j == 7)
         inc(ins, "pe2")
@@ -278,54 +289,61 @@ def rank_program(g, core, T, topo):
         wait(V, "pe2")
         inc(ts(out, T.ps2[:, 0:64], ORIGIN, A.add), name)
 
-    def sums(k, banks, start, stop, names=None):
-        w = R // len(banks)
-        for b, bank in enumerate(banks):
-            ins = PE.matmul(bank[:, 0:w], T.idb[:, :], gat(k, w * b, w * (b + 1)), start, stop)
-            if names:
-                inc(ins, names[b])
+    def add(part, w, x, start=False, stop=None):
+        ins = PE.matmul(part[0], w, x, start, stop is not None)
+        if stop:
+            inc(ins, stop)
 
-    sa, sc = (T.sa0, T.sa1, T.sa2, T.sa3), (T.sc0, T.sc1)
+    def sums(k, parts, start=False):
+        for part in parts:
+            add(part, T.idb[:, :], gat(k, *part[1:]), start)
+
+    sa = [(T["sa%d" % b][:, 0:PARTS[b + 1] - PARTS[b]], PARTS[b], PARTS[b + 1]) for b in range(4)]
+    sc = [(T["sc%d" % b][:, :], 512 * b, 512 * (b + 1)) for b in range(2)]
     p1, p2 = T.mo1[:, 128:256], T.mo1[:, 0:128]
 
-    wait(PE, "cst", "idr", "lt0")
+    wait(PE, "idr", "lt0")
     base([])
-    turned((0, 1), 0)
-    gather(0, split=SPLIT0)
-    wait(V, "ldd")
-    halves(1)
-    wait(PE, "lt1")
-    turned((2, 3), 0)
+    turned(0)
+    gather(0)
+    wait(V, "idr")
+    for j, w in enumerate((2.0, -1.0, 1.0)):
+        inc(ts(T.idh[:, 128 * j:128 * j + 128], T.idb[:, :], w, A.mult), "idw")
     wait(PE, "selr", "rrr")
     slopes(0)
     wait(V, "pe1")
     cells(T.ps1)
     whole(p1)
+    to_partner(T.mi1[:, 128:256], p1, "ex", "am0")
+    to_helpers(3)
     offsets(idx(1), "idxr")
-    wait(PE, "ex")
+    wait(PE, "ex", "idw")
     base([(two, p1)])
-    turned((0, 1), 1)
-    sums(0, sa, True, False)
+    turned(1)
+    sums(0, sa, True)
     gather(1)
     slopes(1)
     wait(V, "pe1")
     whole(p2)
-    to_partner(T.mi1[:, :], T.mo1[:, :], "ex", "am1")
-    sums(1, sa, False, False)
+    to_partner(T.mi1[:, 0:128], p2, "ex", "am1")
+    to_helpers(4)
+    sums(1, sa)
 
     place = {1: T.mi1[:, 128:256], 2: T.mi1[:, 0:128]}
     for k in range(3, 7):
         place[k] = T.pos[:, 128 * (k - 3):128 * (k - 2)]
     wait(V, "am1")
     cells(T.mi1)
-    wait(PE, "ex", "am1")
+    wait(PE, "ex", "am0", "am1")
     for k in range(2, 6):
         offsets(idx(k), "idxr")
         base([(two, place[k]), (minus, place[k - 1])])
         if k > 2:
-            sums(k - 1, sc, k == 3, False)
+            sums(k - 1, sc, k == 3)
         gather(k)
         slopes(k)
+        if k == 5:
+            add(sc[0], T.idb[:, :], gat(5, *sc[0][1:]), stop="c0")
         wait(V, "pe1")
         cells(T.ps1)
         whole(place[k + 1])
@@ -333,46 +351,59 @@ def rank_program(g, core, T, topo):
     offsets(T.mo2[:, :], "m2r")
     to_partner(T.mi2[:, :], T.mo2[:, :], "m2r", "am2")
     base([(two, place[6]), (minus, place[5])], half=False, close=True)
-    sums(5, sc, False, True, ("c0", "c1"))
+    add(sc[1], T.idb[:, :], gat(5, *sc[1][1:]), stop="c1")
     wait(V, "pb")
     inc(V.tensor_copy(T.mo3[:, :], Z), "m3r")
     to_partner(T.mi3[:, :], T.mo3[:, :], "m3r", "am3")
-    for b in range(2):
-        wait(V, "c%d" % b)
-        inc(V.tensor_copy(T.pout[:, 512 * b:512 * (b + 1)], sc[b][:, :]), "pr%d" % b)
-        to_partner(T.pin[:, 512 * b:512 * (b + 1)], T.pout[:, 512 * b:512 * (b + 1)], "pr%d" % b, "ap%d" % b)
+    for j, (a, b) in enumerate(((0, PARTS[1]), (PARTS[1], 512), (512, R))):
+        wait(V, "c%d" % (a // 512))
+        inc(V.tensor_copy(T.pout[:, a:b], T["sc%d" % (a // 512)][:, a % 512:a % 512 + b - a]), "pr%d" % j)
+        to_partner(T.pin[:, a:b], T.pout[:, a:b], "pr%d" % j, "ap%d" % j)
 
+    def partial(b, stop=None):
+        add(sa[b], one, T.pin[:, PARTS[b]:PARTS[b + 1]], stop=stop)
+
+    def last(b):
+        return window(7).indirect(idx(7, PARTS[b] // 16, PARTS[b + 1] // 16))
+
+    def res(b):
+        return T.res[:, PARTS[b]:PARTS[b + 1]]
+
+    def store(q, b, end):
+        wait(q, "cp%d" % b)
+        inc(q.dma_start(T.y[:, PARTS[b]:PARTS[end]], T.res[:, PARTS[b]:PARTS[end]]), "st", 16)
+
+    wait(S, "pe1")
     gather(6, "am2")
     wait(PE, "m2r", "m3r", "am3")
     base([(one, T.mi3[:, :])])
     slopes(6)
+    sums(6, sa[:1])
+    wait(PE, "ap0")
+    partial(0, "a0")
+    wait(S, "a0")
+    inc(S.activation(T.pre[:, :], sa[0][0], COPY), "pre")
     wait(V, "pe1")
     cells(T.ps1)
     offsets(idx(7), "idxr")
-    sums(6, sa, False, False)
+    sums(6, sa[1:])
+    wait(V, "idxr", "pre")
+    inc(V.tensor_tensor(res(0), last(0), T.pre[:, :], A.add), "cp0")
+    inc(V.tensor_copy(gat(7, *sa[3][1:]), last(3)), "g3")
     wait(S, "idxr")
-    wait(V, "idxr")
-    for b in range(4):
-        out, src = gat(7, 256 * b, 256 * (b + 1)), window(7).indirect(idx(7, 16 * b, 16 * (b + 1)))
-        if b % 2 == 0:
-            inc(S.activation(out, src, COPY), "g%d" % b)
-            wait(PE, "ap%d" % (b // 2))
-            for c in (b, b + 1):
-                PE.matmul(sa[c][:, 0:256], one, T.pin[:, 256 * c:256 * (c + 1)], False, False)
-        else:
-            inc(V.tensor_copy(out, src), "g%d" % b)
+    for b in (1, 2):
+        inc(S.activation(gat(7, *sa[b][1:]), last(b), COPY), "g%d" % b)
+        wait(PE, "ap%d" % b)
+        partial(b)
+        if b == 2:
+            partial(3, "a3")
         wait(PE, "g%d" % b)
-        inc(PE.matmul(sa[b][:, 0:256], T.idb[:, :], out, False, True), "a%d" % b)
-    for b in range(4):
-        out, name = T.res[:, 256 * b:256 * (b + 1)], "cpb" if b // 2 else "cpa"
-        if b % 2 == 0:
-            wait(S, "a%d" % b)
-            inc(S.activation(out, sa[b][:, 0:256], COPY), name)
-        else:
-            wait(V, "a%d" % b)
-            inc(V.tensor_copy(out, sa[b][:, 0:256]), name)
-    wait(SY, "cpa")
-    inc(SY.dma_start(T.y[:, 0:512], T.res[:, 0:512]), "st0", 16)
-    wait(S, "cpb")
-    inc(S.dma_start(T.y[:, 512:1024], T.res[:, 512:1024]), "st1", 16)
-    wait(g, "sent", "st0", "st1")
+        add(sa[b], T.idb[:, :], gat(7, *sa[b][1:]), stop="a%d" % b)
+    for b in (1, 2):
+        wait(S, "a%d" % b)
+        inc(S.activation(res(b), sa[b][0], COPY), "cp%d" % b)
+    wait(V, "g3", "a3")
+    inc(V.tensor_tensor(res(3), sa[3][0], gat(7, *sa[3][1:]), A.add), "cp2")
+    for b, end in ((0, 1), (1, 2), (2, 4)):
+        store(SY, b, end)
+    wait(g, "sent", "st")

from concourse.bass import DstId, RemoteDMATransfer
from concourse.mybir import AluOpType, AxisListType, ActivationFunctionType

R, NL = 1024, 64
CELLS = 2048
SEL = 32
TAB = SEL + 2 * CELLS
FIRST = 96
LAST = 1120
HALF = 127.0 / 256.0
SPLIT = 32
PARTS = (0, 256, 512, 736, R)
WHOLE = 2.0 ** 23 + 2048
CELL0 = 2560.0
WRAPX0 = 196608.0
WRAPY0 = 98304.0
WEIGHTS = (1.0 / 16, 4.0, -1.0 / 16, -4.0)
ORIGIN = -(CELL0 / 16 + 4 * CELL0 - WRAPX0 / 16 - 4 * WRAPY0)

SCRATCH = {
    "taba": ("sbuf", [128, TAB], "bfloat16"),
    "tabb": ("sbuf", [128, TAB], "bfloat16"),
    "gat": ("sbuf", [128, 8 * R], "bfloat16"),
    "rays": ("sbuf", [128, 4 * NL], "int32"),
    "faci": ("sbuf", [128, 2], "int32"),
    "facf": ("sbuf", [128, 2], "float32"),
    "iot": ("sbuf", [128, 324], "float32"),
    "selb": ("sbuf", [128, 16], "float32"),
    "e01": ("sbuf", [128, 128], "float32"),
    "e2": ("sbuf", [128, 2, 32], "float32"),
    "mk": ("sbuf", [128, 4], "float32"),
    "eh": ("sbuf", [128, 4, 16], "float16"),
    "kk": ("sbuf", [128, 132], "bfloat16"),
    "cel": ("sbuf", [128, 256], "bfloat16"),
    "rr": ("sbuf", [128, 512], "bfloat16"),
    "idb": ("sbuf", [128, 128], "bfloat16"),
    "idh": ("sbuf", [128, 384], "float16"),
    "hc": ("sbuf", [128, 128], "bfloat16"),
    "lt": ("sbuf", [128, 512], "float16"),
    "idx": ("sbuf", [128, 8 * NL], "uint16"),
    "pos": ("sbuf", [128, 4 * 128], "float16"),
    "cv": ("sbuf", [128, 65, 8], "bfloat16"),
    "mo1": ("sbuf", [128, 256], "float16"),
    "mi1": ("sbuf", [128, 256], "float16"),
    "mo2": ("sbuf", [128, NL], "uint16"),
    "mi2": ("sbuf", [128, NL], "uint16"),
    "mo3": ("sbuf", [128, 128], "float16"),
    "mi3": ("sbuf", [128, 128], "float16"),
    "pout": ("sbuf", [128, R], "float16"),
    "pin": ("sbuf", [128, R], "float16"),
    "pre": ("sbuf", [128, PARTS[1]], "float32"),
    "res": ("sbuf", [128, R], "float32"),
    "sa0": ("psum", [128, 512], "float32"),
    "sa1": ("psum", [128, 512], "float32"),
    "sa2": ("psum", [128, 512], "float32"),
    "sa3": ("psum", [128, 512], "float32"),
    "sc0": ("psum", [128, 512], "float32"),
    "sc1": ("psum", [128, 512], "float32"),
    "ps1": ("psum", [128, 512], "float32"),
    "ps2": ("psum", [128, 512], "float32"),
}
SEMAPHORES = ["ld0", "ld1", "ld2", "ld3", "ldf", "ldp", "ldd", "io0", "io1", "v", "selr", "cst", "idr", "rrr", "lt0",
              "idw", "io2", "fz", "g0", "g1", "g2", "g3",
              "idxr", "gs", "gv", "pe1", "cv0", "cv1", "cv2", "cv3", "ex", "pe2", "pb", "m2r", "m3r", "pr0", "pr1", "c0", "c1",
              "a0", "a1", "a2", "a3", "arr0", "arr1", "am0", "am1", "am2", "am3", "ap0", "ap1", "ap2", "pr2", "sent", "hp0", "hp1", "hp2", "hp3", "hp4",
              "cp0", "cp1", "cp2", "cp3", "pre", "st"]

A = AluOpType
COPY = ActivationFunctionType.Copy


def helpers_of(src, dst, T, topo):
    hs = [h for h in topo.cores_of(src) if T.rank_of(h) is None and topo.may_write(h, dst)]
    far = [h for h in hs if topo.die(h) != topo.die(src)]
    near = [h for h in hs if topo.die(h) == topo.die(src)]
    out = []
    for i in range(max(len(far), len(near))):
        out += far[i:i + 1] + near[i:i + 1]
    return out


def rounds(nh):
    o = CELLS + SEL
    w0, m = (o - FIRST) // (2 * nh), nh // 2
    out = [[(0, 0, FIRST)]]
    out += [[(j, a + w0 * j, a + w0 * (j + 1)) for j in range(nh)] for a in (FIRST, FIRST + nh * w0)]
    for i, (a, w) in enumerate(((o, (CELLS - LAST) // m), (TAB - LAST, LAST // m))):
        out.append([(m * i + j, a + w * j, a + w * (j + 1)) for j in range(m)])
    return out


def carriers(src, helper, partner, i, topo):
    return [e for e in topo.engines(src, helper) if i != 3 or e not in topo.engines(src, partner)]


def helper_program(g, core, T, topo):
    n = len(T.cores)
    for q in range(n):
        src, dst = T.cores[q], T.cores[(q + 1) % n]
        hs = helpers_of(src, dst, T, topo)
        if core not in hs:
            continue
        rid, pid = topo.addr(dst, core)
        sent = 0
        for i, call in enumerate(rounds(len(hs))):
            for j, a, b in call:
                if hs[j] != core:
                    continue
                g.wait_ge(T.sem["hp%d" % i], len(carriers(src, core, T.cores[(q + 2) % n], i, topo)) // len(call))
                g.remote_dma(T.tabb[:, a:b], T.taba[:, a:b], T.sem["arr%d" % (i // 3)], T.sem.sent, pid, rid,
                             topo.mask(core, dst))
                sent += len(topo.engines(core, dst))
        g.wait_ge(T.sem.sent, sent)


def rank_program(g, core, T, topo):
    rank = T.rank_of(core)
    if rank is None:
        helper_program(g, core, T, topo)
        return
    n = len(T.cores)
    nxt, partner, prev = T.cores[(rank + 1) % n], T.cores[(rank + 2) % n], T.cores[(rank - 1) % n]
    V, S, PE, SY = g.vector, g.scalar, g.tensor, g.sync
    cnt = {}

    def inc(ins, name, k=1):
        ins.then_inc(T.sem[name], k)
        cnt[name] = cnt.get(name, 0) + k

    def wait(q, *names):
        for name in names:
            q.wait_ge(T.sem[name], cnt[name])

    def ts(out, in0, s1, op0, s2=None, op1=None):
        if op1 is None:
            return V.tensor_scalar(out, in0, s1, None, op0)
        return V.tensor_scalar(out, in0, s1, s2, op0, op1)

    hs = helpers_of(core, nxt, T, topo)
    calls = rounds(len(hs))

    def load_tab(q, i):
        a, b = calls[i][0][1], min(calls[i][-1][2], CELLS)
        inc(q.dma_start(T.taba[:, a:b], T.lay[:, a:b]), "ld%d" % i, 16)
    inc(V.memset(T.faci[:, :], 0), "fz")
    load_tab(SY, 0)
    for v, src in enumerate((T.px, T.py, T.dx, T.dy)):
        inc((S, SY)[v % 2].dma_start(T.rays[32 * v:32 * v + 32, :], src[:, :]), "ldd" if v // 2 else "ldp", 16)
    wait(S, "fz")
    for uv in range(2):
        inc(S.dma_start(T.faci[14 + uv::16, :], T.fac[14 + uv::16, :]), "ldf", 16)
    load_tab(SY, 1)
    load_tab(SY, 2)
    inc(SY.dma_start(T.taba[:, CELLS + SEL:TAB], T.lay[:, CELLS:2 * CELLS]), "ld3", 16)

    def iota(out, pattern, step, name):
        inc(g.iota(out, pattern, 0, step, allow_small_or_imprecise_dtypes=True), name)
    iota(T.iot[0:64, 192:324], [[1, 132]], -4, "io2")
    iota(T.iot[:, 128:192], [[-1, 2], [-32, 4], [-4, 8]], 1, "io1")
    iota(T.iot[:, 0:128], [[-1, 128]], 1, "io0")
    inc(V.memset(T.cv[:, :, :], 0.0), "cst")
    inc(V.memset(T.hc[:, :], -HALF), "cst")
    wait(V, "io2")
    for v in range(2):
        inc(ts(T.kk[32 * v:32 * v + 32, :], T.iot[32 * v:32 * v + 32, 192:324], 3.0 - 128 * v, A.is_equal, WEIGHTS[v],
               A.mult), "cst")
    wait(V, "io1")
    for h in range(2):
        inc(ts(T.e01[:, 64 * h:64 * h + 64], T.iot[:, 128:192], 2.0 * h, A.is_equal), "v")
    wait(V, "v")
    for h in range(2):
        inc(V.tensor_reduce(T.mk[:, h:h + 1], T.e01[:, 64 * h:64 * h + 64], AxisListType.X, A.add), "v")
    inc(V.tensor_tensor(T.e2[:, :, :], T.e01[:, 0:64], T.e01[:, 64:128], A.add), "v")
    wait(V, "io0")
    inc(ts(T.idb[:, :], T.iot[:, 0:128], 0.0, A.is_equal), "idr")
    for uv in range(2):
        inc(ts(T.selb[:, 8 * uv:8 * uv + 8], T.iot[:, 14 + uv:128:16], 0.0, A.is_equal, 1.0 / 128.0, A.mult), "v")
    wait(V, "v")
    inc(V.tensor_tensor(T.eh[:, 0:2, :], T.e2[:, :, 0:16], T.e2[:, :, 16:32], A.add), "cst")
    inc(ts(T.eh[:, 2:4, :], T.e2[:, :, 0:16], -1.0, A.mult), "cst")
    wait(S, "idr")
    for j, w in enumerate(WEIGHTS):
        inc(S.activation(T.rr[:, 128 * j:128 * j + 128], T.idb[:, :], COPY, scale=w), "rrr")
    two, minus, one = (T.idh[:, 128 * j:128 * j + 128] for j in range(3))

    wait(V, "ldp")
    inc(ts(T.cel[0:64, :], T.rays[0:64, :], CELL0 - 7.5, A.add), "cv0")
    wait(PE, "cst", "cv0")
    for c4 in range(4):
        ins = PE.matmul(T.ps2[:, 0:64], T.kk[0:64, 3 - c4:131 - c4], T.cel[0:64, 64 * c4:64 * c4 + 64], c4 == 0, c4 == 3)
    inc(ins, "pe2")
    wait(V, "ldd")
    inc(ts(T.lt[:, 0::2], T.rays[:, :], T.mk[:, 0:1], A.mult), "lt0")
    wait(V, "pe2")
    inc(ts(T.idx[:, 0:NL], T.ps2[:, 0:64], -CELL0 * (WEIGHTS[0] + WEIGHTS[1]), A.add), "idxr")
    inc(ts(T.lt[:, 1::2], T.rays[:, :], T.mk[:, 1:2], A.mult), "lt0")
    wait(V, "ldf")
    inc(V.tensor_copy(T.facf[:, :], T.faci[:, :]), "v")
    wait(V, "v")
    for l in range(2):
        inc(ts(T.taba[:, CELLS + 16 * l:CELLS + 16 * l + 16], T.selb[:, :], T.facf[:, l:l + 1], A.mult), "selr")

    cnt["sent"] = 0

    def to_helpers(i):
        call = calls[i]
        wait(g, "ld%d" % min(i, 3))
        if i == 2:
            wait(g, "selr")
        trs = []
        for j, (k, a, b) in enumerate(call):
            rid, pid = topo.addr(hs[k], core)
            eng = carriers(core, hs[k], partner, i, topo)[j::len(call)]
            trs.append(RemoteDMATransfer(dst_ids=[DstId(rid=rid, pnc=pid)], dma_engine_mask=sum(1 << e for e in eng),
                                         remote_sem=T.sem["hp%d" % i], src=T.taba[:, a:b], dst=T.taba[:, a:b]))
            cnt["sent"] += len(eng)
        g.remote_dma_fused(trs, local_sem=T.sem.sent)
    for i in range(3):
        to_helpers(i)
    hp = helpers_of(prev, core, T, topo)
    for lay in range(2):
        cnt["arr%d" % lay] = sum(len(topo.engines(hp[k], core)) for call in calls[3 * lay:3 * lay + 3] for k, a, b in call)
    for name in ("am0", "am1", "am2", "am3", "ap0", "ap1", "ap2"):
        cnt[name] = len(topo.engines(partner, core))
    prid, ppid = topo.addr(partner, core)

    def to_partner(dst, src, ready, arrive):
        wait(g, ready)
        g.remote_dma(dst, src, T.sem[arrive], T.sem.sent, ppid, prid, topo.mask(core, partner))
        cnt["sent"] += len(topo.engines(core, partner))

    where = [(T.taba, 0, ("ld0", "ld1", "ld2")), (T.taba, 1, ("ld3",)), (T.tabb, 0, ("arr0",)), (T.tabb, 1, ("arr1",)),
             (T.taba, 0, ()), (T.taba, 1, ()), (T.tabb, 0, ()), (T.tabb, 1, ())]
    Z = T.ps1[:, 0:128]

    def window(k):
        tab, l, need = where[k]
        return tab[:, (SEL + CELLS) * l:(SEL + CELLS) * l + CELLS]

    def idx(k, a=0, b=NL):
        return T.mi2[:, a:b] if k == 6 else T.idx[:, NL * k + a:NL * k + b]

    def gat(k, a, b):
        return T.gat[:, R * k + a:R * k + b]

    def gather(k, ready="idxr", split=SPLIT):
        wait(S, *where[k][2], ready)
        inc(S.activation(gat(k, 0, 16 * split), window(k).indirect(idx(k, 0, split)), COPY), "gs")
        wait(V, *where[k][2], ready)
        inc(V.tensor_copy(gat(k, 16 * split, R), window(k).indirect(idx(k, split, NL))), "gs")

    def base(terms, half=True, close=False):
        if half:
            terms = [(T.idb[:, :], T.hc[:, :])] + terms
        for j, (w, x) in enumerate(terms):
            ins = PE.matmul(Z, w, x, j == 0, close and j == len(terms) - 1)
        inc(ins, "pb")

    def turned(j):
        wait(PE, "pb")
        for ch in range(8):
            inc(PE.matmul(T.ps1[:, ch:128:8], T.lt[:, 128 * (ch % 4):128 * (ch % 4) + 128], T.eh[:, 2 * j + ch // 4, :],
                          False, False), "pb")

    def slopes(k):
        tab, l, need = where[k]
        wait(PE, "pb", "gs")
        for ch in range(8):
            inc(PE.matmul(T.ps1[:, ch:128:8], T.gat[:, R * k + ch:R * (k + 1):8],
                          tab[:, CELLS + 16 * l:CELLS + 16 * l + 16], False, ch == 7), "pe1")

    def cells(z):
        inc(ts(T.cv[:, 1:17:2, :], z[:, 0:64], CELL0 - 7.5, A.add), "cv0")
        inc(ts(T.cv[:, 17:33:2, :], z[:, 64:128], CELL0 - 7.5, A.add), "cv1")
        inc(ts(T.cv[:, 33:49:2, :], z[:, 0:64], WHOLE, A.add, WHOLE - (WRAPX0 - 511.5), A.subtract), "cv2")
        inc(ts(T.cv[:, 49:65:2, :], z[:, 64:128], WHOLE, A.add, WHOLE - (WRAPY0 - 255.5), A.subtract), "cv3")
        for j in range(8):
            c, h = j // 2, j % 2
            if h == 0:
                wait(PE, "cv%d" % c)
            b = 16 * c + 1 - h
            ins = PE.matmul(T.ps2[:, 0:64], T.cv[:, b:b + 16, :], T.rr[:, 128 * c + h:128 * c + 128:2], j == 0, j == 7)
        inc(ins, "pe2")

    def whole(out):
        inc(ts(out, Z, WHOLE, A.add, WHOLE, A.subtract), "ex")

    def offsets(out, name):
        wait(V, "pe2")
        inc(ts(out, T.ps2[:, 0:64], ORIGIN, A.add), name)

    def add(part, w, x, start=False, stop=None):
        ins = PE.matmul(part[0], w, x, start, stop is not None)
        if stop:
            inc(ins, stop)

    def sums(k, parts, start=False):
        for part in parts:
            add(part, T.idb[:, :], gat(k, *part[1:]), start)

    sa = [(T["sa%d" % b][:, 0:PARTS[b + 1] - PARTS[b]], PARTS[b], PARTS[b + 1]) for b in range(4)]
    sc = [(T["sc%d" % b][:, :], 512 * b, 512 * (b + 1)) for b in range(2)]
    p1, p2 = T.mo1[:, 128:256], T.mo1[:, 0:128]

    wait(PE, "idr", "lt0")
    base([])
    turned(0)
    gather(0)
    wait(V, "idr")
    for j, w in enumerate((2.0, -1.0, 1.0)):
        inc(ts(T.idh[:, 128 * j:128 * j + 128], T.idb[:, :], w, A.mult), "idw")
    wait(PE, "selr", "rrr")
    slopes(0)
    wait(V, "pe1")
    cells(T.ps1)
    whole(p1)
    to_partner(T.mi1[:, 128:256], p1, "ex", "am0")
    to_helpers(3)
    offsets(idx(1), "idxr")
    wait(PE, "ex", "idw")
    base([(two, p1)])
    turned(1)
    sums(0, sa, True)
    gather(1)
    slopes(1)
    wait(V, "pe1")
    whole(p2)
    to_partner(T.mi1[:, 0:128], p2, "ex", "am1")
    to_helpers(4)
    sums(1, sa)

    place = {1: T.mi1[:, 128:256], 2: T.mi1[:, 0:128]}
    for k in range(3, 7):
        place[k] = T.pos[:, 128 * (k - 3):128 * (k - 2)]
    wait(V, "am1")
    cells(T.mi1)
    wait(PE, "ex", "am0", "am1")
    for k in range(2, 6):
        offsets(idx(k), "idxr")
        base([(two, place[k]), (minus, place[k - 1])])
        if k > 2:
            sums(k - 1, sc, k == 3)
        gather(k)
        slopes(k)
        if k == 5:
            add(sc[0], T.idb[:, :], gat(5, *sc[0][1:]), stop="c0")
        wait(V, "pe1")
        cells(T.ps1)
        whole(place[k + 1])
        wait(PE, "ex")
    offsets(T.mo2[:, :], "m2r")
    to_partner(T.mi2[:, :], T.mo2[:, :], "m2r", "am2")
    base([(two, place[6]), (minus, place[5])], half=False, close=True)
    add(sc[1], T.idb[:, :], gat(5, *sc[1][1:]), stop="c1")
    wait(V, "pb")
    inc(V.tensor_copy(T.mo3[:, :], Z), "m3r")
    to_partner(T.mi3[:, :], T.mo3[:, :], "m3r", "am3")
    for j, (a, b) in enumerate(((0, PARTS[1]), (PARTS[1], 512), (512, R))):
        wait(V, "c%d" % (a // 512))
        inc(V.tensor_copy(T.pout[:, a:b], T["sc%d" % (a // 512)][:, a % 512:a % 512 + b - a]), "pr%d" % j)
        to_partner(T.pin[:, a:b], T.pout[:, a:b], "pr%d" % j, "ap%d" % j)

    def partial(b, stop=None):
        add(sa[b], one, T.pin[:, PARTS[b]:PARTS[b + 1]], stop=stop)

    def last(b):
        return window(7).indirect(idx(7, PARTS[b] // 16, PARTS[b + 1] // 16))

    def res(b):
        return T.res[:, PARTS[b]:PARTS[b + 1]]

    def store(q, b, end):
        wait(q, "cp%d" % b)
        inc(q.dma_start(T.y[:, PARTS[b]:PARTS[end]], T.res[:, PARTS[b]:PARTS[end]]), "st", 16)

    wait(S, "pe1")
    gather(6, "am2")
    wait(PE, "m2r", "m3r", "am3")
    base([(one, T.mi3[:, :])])
    slopes(6)
    sums(6, sa[:1])
    wait(PE, "ap0")
    partial(0, "a0")
    wait(S, "a0")
    inc(S.activation(T.pre[:, :], sa[0][0], COPY), "pre")
    wait(V, "pe1")
    cells(T.ps1)
    offsets(idx(7), "idxr")
    sums(6, sa[1:])
    wait(V, "idxr", "pre")
    inc(V.tensor_tensor(res(0), last(0), T.pre[:, :], A.add), "cp0")
    inc(V.tensor_copy(gat(7, *sa[3][1:]), last(3)), "g3")
    wait(S, "idxr")
    for b in (1, 2):
        inc(S.activation(gat(7, *sa[b][1:]), last(b), COPY), "g%d" % b)
        wait(PE, "ap%d" % b)
        partial(b)
        if b == 2:
            partial(3, "a3")
        wait(PE, "g%d" % b)
        add(sa[b], T.idb[:, :], gat(7, *sa[b][1:]), stop="a%d" % b)
    for b in (1, 2):
        wait(S, "a%d" % b)
        inc(S.activation(res(b), sa[b][0], COPY), "cp%d" % b)
    wait(V, "g3", "a3")
    inc(V.tensor_tensor(res(3), sa[3][0], gat(7, *sa[3][1:]), A.add), "cp2")
    for b, end in ((0, 1), (1, 2), (2, 4)):
        store(SY, b, end)
    wait(g, "sent", "st")
